import numpy as np
import ml_dtypes


def mxq(x, axis, fmt="e4m3"):
    dtype, down = {"e4m3": (ml_dtypes.float8_e4m3fn, 7), "e5m2": (ml_dtypes.float8_e5m2, 14)}[fmt]
    v = np.moveaxis(np.asarray(x, np.float32).astype(ml_dtypes.bfloat16).astype(np.float64), axis, -1)
    blocks = v.reshape(v.shape[:-1] + (-1, 32))
    amax = np.abs(blocks).max(-1, keepdims=True)
    byte = np.maximum(np.where(amax > 0, np.frexp(amax)[1] - 1 + 127, 0) - down, 1)
    scale = np.exp2(byte - 127.0)
    codes = (blocks / scale).astype(np.float32).astype(dtype).astype(np.float64)
    return np.moveaxis((codes * scale).reshape(v.shape), -1, axis)


WIDE = False


def mx_kscale(k):
    if not WIDE:
        return np.ones(k)
    levels = np.array([10, -10, 5, -5, 0])
    if k % 512:
        return np.exp2(np.random.permutation(np.resize(levels, k // 32))).repeat(32)
    a = np.empty((k // 512, 16))
    for p in range(k // 512):
        a[p, :8] = np.random.permutation(np.resize(levels, 8))
        for g in range(8):
            far = levels[np.abs(levels - a[p, g]) >= 10]
            a[p, g + 8] = far[np.random.randint(len(far))]
    return np.exp2(a.ravel()).repeat(32)


BF16 = ml_dtypes.bfloat16


def bf(x):
    return np.asarray(x, np.float32).astype(BF16)


def f64(x):
    return np.asarray(x).astype(np.float64)


E2M1 = np.array([0.0, 0.5, 1.0, 1.5, 2.0, 3.0, 4.0, 6.0, -0.0, -0.5, -1.0, -1.5, -2.0, -3.0, -4.0, -6.0])


def pack_weight(w, fmt):
    k, n = w.shape
    w = f64(bf(w)).reshape(k // 32, 32, n)
    amax = np.abs(w).max(1)
    if fmt == "e4m3":
        byte = np.frexp(amax)[1] - 1 + 127 - 7
    else:
        mant, ex = np.frexp(amax / 6.0)
        byte = np.where(mant > 0.5, ex, ex - 1) + 127
    byte = np.clip(np.where(amax > 0, byte, 1), 1, 254)
    scaled = (w * np.exp2(127.0 - byte)[:, None, :]).reshape(k, n).astype(np.float32)
    by_word = np.ascontiguousarray(scaled.reshape(k // 512, 128, 4, n).transpose(0, 1, 3, 2))
    if fmt == "e4m3":
        words = by_word.astype(ml_dtypes.float8_e4m3fn).view(np.uint8)
    else:
        c = by_word.astype(ml_dtypes.float4_e2m1fn).view(np.uint8) & 0xF
        words = c[..., 0::2] | (c[..., 1::2] << 4)
    return np.ascontiguousarray(words), np.ascontiguousarray(byte.astype(np.uint8).reshape(k // 512, 16, n))


def unpack_weight(words, scales, fmt):
    g, p, n, _ = words.shape
    if fmt == "e4m3":
        vals = np.ascontiguousarray(words).view(ml_dtypes.float8_e4m3fn).astype(np.float64)
    else:
        nib = np.empty((g, p, n, 4), np.uint8)
        nib[..., 0::2] = words & 0xF
        nib[..., 1::2] = words >> 4
        vals = E2M1[nib]
    vals = vals * np.repeat(np.exp2(scales.astype(np.float64) - 127.0), 8, axis=1)[..., None]
    return vals.transpose(0, 1, 3, 2).reshape(g * 512, n)
def pack4(w):
    words, scales = pack_weight(w, "e2m1")
    return words.reshape(words.shape[0], 128, -1), scales


def unpack4(words, scales):
    return unpack_weight(words.reshape(words.shape[0], 128, -1, 2), scales, "e2m1")


E4M3FN = np.array([(-1.0 if i & 128 else 1.0) * ((1.0 + (i & 7) / 8.0) * 2.0 ** (((i >> 3) & 15) - 7) if i & 120 else (i & 7) * 2.0 ** -9) for i in range(256)])


def e4m3fn_bytes(y):
    return np.clip(np.asarray(y, np.float64), -448.0, 448.0).astype(np.float32).astype(ml_dtypes.float8_e4m3fn).view(np.uint8)


def e4m3fn_values(b):
    return E4M3FN[b]


T, N, M, R, B = 1024, 2048, 1024, 512, 128


def setup_inputs():
    s, t = mx_kscale(M), mx_kscale(N)
    x = np.random.standard_normal((T, M)) * M ** 0.25
    y = np.random.standard_normal((N, M)) * M ** 0.25
    x = (x - x.mean(1, keepdims=True)) * s
    y = (y - y.mean(1, keepdims=True)) / s
    x_scale = (np.abs(x).reshape(T, M // B, B).max(2) / 448).astype(np.float32)
    y_scale = (np.abs(y).reshape(N // B, B, M // B, B).max((1, 3)) / 448).astype(np.float32)
    x_bytes = e4m3fn_bytes(x / np.repeat(f64(x_scale), B, 1))
    y_bytes = e4m3fn_bytes(y / np.repeat(np.repeat(f64(y_scale), B, 0), B, 1))
    a, b = 2 * np.random.random(T), 2 * np.random.random(N)
    rho = np.exp(-np.abs(a[:, None] - b)) * t
    h_words, h_scales = pack4(np.random.standard_normal((N, R)) / np.sqrt(N) / t[:, None])
    return {"x_bytes": x_bytes, "x_scale": x_scale, "y_bytes": y_bytes, "y_scale": y_scale,
            "rho": bf(rho), "h_words": h_words, "h_scales": h_scales}


def reference(x_bytes, x_scale, y_bytes, y_scale, rho, h_words, h_scales):
    x = e4m3fn_values(x_bytes) * np.repeat(f64(x_scale), B, 1)
    y = e4m3fn_values(y_bytes) * np.repeat(np.repeat(f64(y_scale), B, 0), B, 1)
    c = (mxq(x, 1, "e4m3") @ mxq(y, 1, "e4m3").T) / (M - 1)
    z = c * f64(rho)
    return mxq(z, 1, "e4m3") @ unpack4(h_words, h_scales)

@@ -1,0 +1,320 @@
+from contextlib import ExitStack
+
+import concourse.mybir as mybir
+from concourse.masks import make_identity
+
+T, N, M, R = 1024, 2048, 1024, 512
+P = 128
+FLOPS = 2 * T * N * M + 2 * T * N * R
+
+F32 = mybir.dt.float32
+BF16 = mybir.dt.bfloat16
+I32 = mybir.dt.int32
+U32 = mybir.dt.uint32
+U8 = mybir.dt.uint8
+FP8 = mybir.dt.float8_e4m3fn
+FP8X4 = mybir.dt.float8_e4m3fn_x4
+FP4X4 = mybir.dt.float4_e2m1fn_x4
+MULT = mybir.AluOpType.mult
+COPY = mybir.ActivationFunctionType.Copy
+
+STEPS = [
+    ((("y", 0), ("x", 3)), (), 0),
+    ((("y", 1), ("x", 1)), (), 0),
+    ((("x", 2), ("x", 0)), (), 1),
+    ((), ((3, 0), (1, 0)), 2),
+    ((("y", 3),), ((2, 0), (0, 0)), 1),
+    ((("y", 2), ("y", 4)), (), 1),
+    ((), ((1, 1), (0, 1)), 1),
+    ((("y", 5),), ((2, 1),), 2),
+    ((), ((3, 1), (1, 2)), 0),
+    ((("y", 6),), ((3, 2), (0, 2)), 2),
+    ((("y", 7),), (), 1),
+    ((), ((3, 3),), 2),
+    ((), ((1, 3), (2, 2)), 1),
+    ((), ((0, 3),), 0),
+    ((), ((2, 3),), 1),
+]
+
+WIDENED_BY = {
+    ("x", 0): ("vv", "sv"),
+    ("x", 1): ("vs", "sv"),
+    ("x", 2): ("vv", "vv"),
+    ("x", 3): ("ss", "vv"),
+    ("y", 0): ("vs", "sv"),
+    ("y", 1): ("vv", "vv"),
+    ("y", 2): ("vs", "ss"),
+    ("y", 3): ("sv", "vv"),
+    ("y", 4): ("ss", "ss"),
+    ("y", 5): ("vs", "ss"),
+    ("y", 6): ("ss", "ss"),
+    ("y", 7): ("ss", "vs"),
+}
+
+
+def tile_localised_ensemble_covariance_d4_kernel(tc, x_bytes, x_scale, y_bytes, y_scale, rho, h_words, h_scales, out):
+    nc = tc.nc
+    with ExitStack() as ctx:
+        keep = ctx.enter_context(tc.tile_pool(name="keep", bufs=1))
+        wide_pool = ctx.enter_context(tc.tile_pool(name="wide", bufs=8))
+        stage = ctx.enter_context(tc.tile_pool(name="stage", bufs=4))
+        psum_turn = ctx.enter_context(tc.psum_pool(name="psum_turn", bufs=4))
+        psum_acc = ctx.enter_context(tc.psum_pool(name="psum_acc", bufs=4))
+        ctx.enter_context(tc.manual_schedule())
+
+        y_scales = keep.tile([P, 16, 8], F32, name="y_scales")
+        nc.scalar.dma_start(out=y_scales[:].rearrange("p b k -> p (b k)"), in_=y_scale.rearrange("b k -> (b k)").partition_broadcast(P))
+        x_scales = keep.tile([P, 8, 8], F32, name="x_scales")
+        nc.scalar.dma_start(out=x_scales[:], in_=x_scale.rearrange("(i p) k -> p i k", p=P))
+
+        byte_rows = {"x": x_bytes.rearrange("(i p) k -> p i k", p=P), "y": y_bytes.rearrange("(i p) k -> p i k", p=P)}
+        rho_rows = rho.rearrange("(i p) n -> p i n", p=P)
+        raw = {}
+        weights = {}
+        first_pair = STEPS[0][0][0]
+        for pairs, panels, n_out in STEPS:
+            for kind, j in pairs:
+                raw_pair = keep.tile([P, 2, M], U8, name=f"raw_{kind}{j}")
+                if (kind, j) == first_pair:
+                    for a in range(2):
+                        nc.sync.dma_start(out=raw_pair[:, a, :], in_=byte_rows[kind][:, 2 * j + a, :])
+                else:
+                    nc.sync.dma_start(out=raw_pair[:], in_=byte_rows[kind][:, 2 * j : 2 * j + 2, :])
+                raw[kind, j] = raw_pair
+            for q, g in panels:
+                weights_panel = keep.tile([P, 2, 512], BF16, name=f"rho_{q}{g}")
+                nc.sync.dma_start(out=weights_panel[:], in_=rho_rows[:, 2 * q : 2 * q + 2, 512 * g : 512 * g + 512])
+                weights[q, g] = weights_panel
+        h_codes = keep.tile([P, 4, 2 * R], U8, name="h_codes", align_bytes=64)
+        nc.sync.dma_start(out=h_codes[:].bitcast(I32), in_=h_words.rearrange("g p c -> p g c").bitcast(I32))
+        h_plane = keep.tile([P, 4, R], U8, name="h_plane", align_bytes=64)
+        nc.gpsimd.memset(h_plane[:].bitcast(I32), 0)
+        for quad in range(4):
+            nc.sync.dma_start(
+                out=h_plane[32 * quad : 32 * quad + 4, :, :].bitcast(I32),
+                in_=h_scales[:, 4 * quad : 4 * quad + 4, :].rearrange("g r n -> r g n").bitcast(I32),
+            )
+
+        identity = keep.tile([P, P], F32, name="identity")
+        make_identity(nc, identity[:])
+
+        codes = {}
+        planes = {}
+
+        def operand(key, shape, name):
+            codes[key] = keep.tile(shape, U32, name=f"codes_{name}", align_bytes=64)
+            planes[key] = keep.tile(shape, U8, name=f"plane_{name}", align_bytes=64)
+
+        for g in range(4):
+            operand(("y", g), [P, 2, 512], f"y{g}")
+        for q in range(4):
+            operand(("x", q), [P, 2, 256], f"x{q}")
+            for g in range(4):
+                operand(("z", q, g), [P, 256], f"z{q}{g}")
+
+        widened = {}
+        grouped = {}
+
+        def widen(pair):
+            kind, j = pair
+            scale_tile = x_scales if kind == "x" else y_scales
+            widened[pair] = [wide_pool.tile([P, 2, 512], BF16, name="wide", align_bytes=64) for a in range(2)]
+            for engine in "vs":
+                for a in range(2):
+                    wide = widened[pair][a]
+                    for g in range(2):
+                        if WIDENED_BY[pair][a][g] != engine:
+                            continue
+                        for b in range(4):
+                            m0 = 512 * g + 128 * b
+                            values = raw[pair][:, a, m0 : m0 + 128].bitcast(FP8)
+                            scale = scale_tile[:, 2 * j + a, m0 // 128 : m0 // 128 + 1]
+                            if engine == "v":
+                                by_word = wide[:, g, :].rearrange("r (u p e) -> r p u e", u=2, e=2)
+                                nc.vector.tensor_scalar(
+                                    out=by_word[:, 32 * b : 32 * b + 32, :, :],
+                                    in0=values.rearrange("r (p u e) -> r p u e", u=2, e=2),
+                                    scalar1=scale,
+                                    scalar2=None,
+                                    op0=MULT,
+                                )
+                            else:
+                                nc.scalar.activation(out=wide[:, g, 128 * b : 128 * b + 128], in_=values, func=COPY, scale=scale)
+
+        def turn_pair(pair):
+            banks = []
+            for a in range(2):
+                bank = psum_turn.tile([P, 2, 2, P], F32, name="turn")
+                words = widened[pair][a][:].bitcast(F32)
+                for g in range(2):
+                    for u in range(2):
+                        if WIDENED_BY[pair][a][g] == "v":
+                            part = words[:, g, 128 * u : 128 * u + 128]
+                        else:
+                            part = words[:, g, u : 256 : 2]
+                        nc.tensor.transpose(bank[:, g, u, :], part, identity[:])
+                banks.append(bank)
+            return banks
+
+        def empty_pair(pair, banks):
+            grouped[pair] = stage.tile([P, 2, 2, P, 4], BF16, name="grouped", align_bytes=64)
+            for a in range(2):
+                nc.scalar.copy(out=grouped[pair][:, :, a, :, :].bitcast(F32), in_=banks[a][:].rearrange("p g u r -> p g r u"))
+
+        def quantise_pair(pair):
+            kind, j = pair
+            if kind == "x":
+                nc.vector.quantize_mx(
+                    out=codes["x", j][:].rearrange("p g r -> p (g r)").bitcast(FP8X4),
+                    scales=planes["x", j][:].rearrange("p g r -> p (g r)"),
+                    in_=grouped[pair][:].rearrange("p g a r t -> p (g a r t)"),
+                )
+                return
+            rows = slice(256 * (j % 2), 256 * (j % 2) + 256)
+            for g in range(2):
+                nc.vector.quantize_mx(
+                    out=codes["y", j // 2][:, g, rows].bitcast(FP8X4),
+                    scales=planes["y", j // 2][:, g, rows],
+                    in_=grouped[pair][:, g, :, :, :].rearrange("p a r t -> p (a r t)"),
+                )
+
+        def first_product(q, g):
+            banks = []
+            for a in range(2):
+                acc = psum_acc.tile([P, 512], F32, name="acc")
+                rows = slice(128 * a, 128 * a + 128)
+                for k in range(2):
+                    nc.tensor.matmul_mx(
+                        out=acc[:],
+                        lhsT=codes["x", q][:, k, rows].bitcast(FP8X4),
+                        lhsT_scale=planes["x", q][:, k, rows],
+                        rhs=codes["y", g][:, k, :].bitcast(FP8X4),
+                        rhs_scale=planes["y", g][:, k, :],
+                        start=(k == 0),
+                        stop=(k == 1),
+                    )
+                banks.append(acc)
+            return banks
+
+        def localise(q, g, banks):
+            tiles = []
+            for a in range(2):
+                z = stage.tile([P, 2, 256], BF16, name=f"z{a}", align_bytes=64)
+                for u in range(2):
+                    nc.vector.scalar_tensor_tensor(
+                        out=z[:, u, :].rearrange("r (p e) -> r p e", e=2),
+                        in0=banks[a][:].rearrange("r (p u e) -> r u p e", u=2, e=2)[:, u, :, :],
+                        scalar=1.0 / (M - 1),
+                        in1=weights[q, g][:, a, :].rearrange("r (p u e) -> r u p e", u=2, e=2)[:, u, :, :],
+                        op0=MULT,
+                        op1=MULT,
+                    )
+                tiles.append(z)
+            return tiles
+
+        def turn_panel(tiles):
+            bank = psum_turn.tile([P, 2, 2, P], F32, name="turn")
+            for a in range(2):
+                words = tiles[a][:].bitcast(F32)
+                for u in range(2):
+                    nc.tensor.transpose(bank[:, a, u, :], words[:, u, :], identity[:])
+            return bank
+
+        def empty_panel(bank):
+            z_grouped = stage.tile([P, 2, P, 4], BF16, name="z_grouped", align_bytes=64)
+            nc.scalar.copy(out=z_grouped[:].bitcast(F32), in_=bank[:].rearrange("p a u r -> p a r u"))
+            return z_grouped
+
+        def quantise_panel(q, g, z_grouped):
+            nc.vector.quantize_mx(
+                out=codes["z", q, g][:].bitcast(FP8X4),
+                scales=planes["z", q, g][:],
+                in_=z_grouped[:].rearrange("p a r t -> p (a r t)"),
+            )
+
+        def second_pass(i, g, acc, start, stop):
+            q, a = divmod(i, 2)
+            rows = slice(128 * a, 128 * a + 128)
+            nc.tensor.matmul_mx(
+                out=acc[:],
+                lhsT=codes["z", q, g][:, rows].bitcast(FP8X4),
+                lhsT_scale=planes["z", q, g][:, rows],
+                rhs=h_codes[:, g, :].bitcast(FP4X4),
+                rhs_scale=h_plane[:, g, :],
+                start=start,
+                stop=stop,
+            )
+
+        def second_product(i):
+            acc = psum_acc.tile([P, R], F32, name="acc")
+            for g in range(4):
+                second_pass(i, g, acc, g == 0, g == 3)
+            return acc
+
+        def store(i, acc, on_vector=False):
+            rows = stage.tile([P, R], F32, name="out_rows")
+            if on_vector:
+                nc.vector.tensor_copy(out=rows[:], in_=acc[:])
+            else:
+                nc.scalar.copy(out=rows[:], in_=acc[:])
+            nc.sync.dma_start(out=out[128 * i : 128 * i + 128, :], in_=rows[:])
+
+        last_q = STEPS[-1][1][-1][0]
+        n_steps = len(STEPS)
+        steps = STEPS + [((), (), 2), ((), (), 8), ((), (), 8)]
+        turned_pairs = []
+        turned_panels = []
+        localised = []
+        panels_missing = [4, 4, 4, 4]
+        ready = []
+        summed = []
+        last_acc = []
+        last_panels = []
+        n_summed = 0
+        for pair in STEPS[0][0]:
+            widen(pair)
+        for s, (pairs, panels, n_out) in enumerate(steps):
+            for pair in steps[s + 1][0] if s + 1 < len(steps) else ():
+                widen(pair)
+            for pair in turned_pairs:
+                quantise_pair(pair)
+            for q, g, z_grouped in turned_panels:
+                quantise_panel(q, g, z_grouped)
+                panels_missing[q] -= 1
+                if q == last_q:
+                    last_panels.append(g)
+                elif panels_missing[q] == 0:
+                    ready.extend([2 * q, 2 * q + 1])
+
+            pair_banks = [turn_pair(pair) for pair in pairs]
+            due = [entry for entry in localised if entry[0] <= s - 2 or s >= n_steps]
+            if s >= n_steps:
+                due = due[:2]
+            localised = [entry for entry in localised if entry not in due]
+            panel_banks = [turn_panel(tiles) for made, q, g, tiles in due]
+            for pair, banks in zip(pairs, pair_banks):
+                empty_pair(pair, banks)
+            turned_pairs = pairs
+            turned_panels = [(q, g, empty_panel(bank)) for (made, q, g, tiles), bank in zip(due, panel_banks)]
+            for i, acc in summed:
+                store(i, acc)
+
+            products = [first_product(q, g) for q, g in panels]
+            summed = [(i, second_product(i)) for i in ready[:n_out]]
+            ready = ready[n_out:]
+            if s > n_steps and last_panels:
+                if not last_acc:
+                    for a in range(2):
+                        acc = psum_acc.tile([P, R], F32, name="acc")
+                        last_acc.append(acc)
+                for a in range(2):
+                    for n, g in enumerate(last_panels, n_summed):
+                        second_pass(2 * last_q + a, g, last_acc[a], n == 0, n == 3)
+                n_summed += len(last_panels)
+                last_panels = []
+                if n_summed == 4:
+                    summed.extend((2 * last_q + a, last_acc[a]) for a in range(2))
+            for (q, g), banks in zip(panels, products):
+                localised.append((s, q, g, localise(q, g, banks)))
+        for n, (i, acc) in enumerate(summed):
+            store(i, acc, on_vector=(n == 0))

@@ -18,303 +18,277 @@ FP4X4 = mybir.dt.float4_e2m1fn_x4
 MULT = mybir.AluOpType.mult
 COPY = mybir.ActivationFunctionType.Copy
 
-STEPS = [
-    ((("y", 0), ("x", 3)), (), 0),
-    ((("y", 1), ("x", 1)), (), 0),
-    ((("x", 2), ("x", 0)), (), 1),
-    ((), ((3, 0), (1, 0)), 2),
-    ((("y", 3),), ((2, 0), (0, 0)), 1),
-    ((("y", 2), ("y", 4)), (), 1),
-    ((), ((1, 1), (0, 1)), 1),
-    ((("y", 5),), ((2, 1),), 2),
-    ((), ((3, 1), (1, 2)), 0),
-    ((("y", 6),), ((3, 2), (0, 2)), 2),
-    ((("y", 7),), (), 1),
-    ((), ((3, 3),), 2),
-    ((), ((1, 3), (2, 2)), 1),
-    ((), ((0, 3),), 0),
-    ((), ((2, 3),), 1),
-]
-
-WIDENED_BY = {
-    ("x", 0): ("vv", "sv"),
-    ("x", 1): ("vs", "sv"),
-    ("x", 2): ("vv", "vv"),
-    ("x", 3): ("ss", "vv"),
-    ("y", 0): ("vs", "sv"),
-    ("y", 1): ("vv", "vv"),
-    ("y", 2): ("vs", "ss"),
-    ("y", 3): ("sv", "vv"),
-    ("y", 4): ("ss", "ss"),
-    ("y", 5): ("vs", "ss"),
-    ("y", 6): ("ss", "ss"),
-    ("y", 7): ("ss", "vs"),
-}
+PAIRS = [("x",0),("y", 0, 0), ("y", 0, 1),("x",1),("x",2),("x",3),("y", 1, 0), ("y", 1, 1),("y", 2, 0), ("y", 2, 1),("y", 3, 0), ("y", 3, 1)]
+TURN_STEP = dict(zip(PAIRS, [0,0,1,1,2,3,3,4,5,6,7,8]))
+PANELS = [(q,g) for g in range(4) for q in range(4)]
+PANEL_STEP = dict(zip(PANELS, [2,3,4,5,6,6,7,7,8,8,9,9,10,10,11,11]))
+LAST_STEP = max(PANEL_STEP.values())
+CAST_FIRST = [p for p in PAIRS if p[0]=="y"]
 
 
 def tile_localised_ensemble_covariance_d4_kernel(tc, x_bytes, x_scale, y_bytes, y_scale, rho, h_words, h_scales, out):
     nc = tc.nc
     with ExitStack() as ctx:
         keep = ctx.enter_context(tc.tile_pool(name="keep", bufs=1))
-        wide_pool = ctx.enter_context(tc.tile_pool(name="wide", bufs=8))
-        stage = ctx.enter_context(tc.tile_pool(name="stage", bufs=4))
+        stage = ctx.enter_context(tc.tile_pool(name="stage", bufs=3))
+        z_pool = ctx.enter_context(tc.tile_pool(name="z_pool", bufs=6))
         psum_turn = ctx.enter_context(tc.psum_pool(name="psum_turn", bufs=4))
         psum_acc = ctx.enter_context(tc.psum_pool(name="psum_acc", bufs=4))
         ctx.enter_context(tc.manual_schedule())
 
-        y_scales = keep.tile([P, 16, 8], F32, name="y_scales")
-        nc.scalar.dma_start(out=y_scales[:].rearrange("p b k -> p (b k)"), in_=y_scale.rearrange("b k -> (b k)").partition_broadcast(P))
         x_scales = keep.tile([P, 8, 8], F32, name="x_scales")
-        nc.scalar.dma_start(out=x_scales[:], in_=x_scale.rearrange("(i p) k -> p i k", p=P))
+        nc.scalar.dma_start(out=x_scales[:], in_=x_scale.rearrange("(p i) k -> p i k", p=P))
+        all_y_scales = keep.tile([P, 4, 4, 8], F32, name="all_y_scales")
+        nc.scalar.dma_start(out=all_y_scales[:].rearrange("p g quad k -> p (g quad k)"), in_=y_scale.rearrange("b k -> (b k)").partition_broadcast(P))
+        y_scales = keep.tile([P, 4, 8], F32, name="y_scales")
+        for quad in range(4):
+            nc.scalar.copy(out=y_scales[32 * quad : 32 * quad + 32, :, :], in_=all_y_scales[32 * quad : 32 * quad + 32, :, quad, :])
 
-        byte_rows = {"x": x_bytes.rearrange("(i p) k -> p i k", p=P), "y": y_bytes.rearrange("(i p) k -> p i k", p=P)}
-        rho_rows = rho.rearrange("(i p) n -> p i n", p=P)
+        x_rows = x_bytes.rearrange("(p q a) k -> q p a k", a=2, p=P)
+        y_rows = y_bytes.rearrange("(g p u e) k -> g u p e k", p=P, u=2, e=2)
+        rho_rows = rho.rearrange("(p q a) n -> q p a n", a=2, p=P)
+        out_rows = out.rearrange("(p i) r -> i p r", p=P)
         raw = {}
         weights = {}
-        first_pair = STEPS[0][0][0]
-        for pairs, panels, n_out in STEPS:
-            for kind, j in pairs:
-                raw_pair = keep.tile([P, 2, M], U8, name=f"raw_{kind}{j}")
-                if (kind, j) == first_pair:
-                    for a in range(2):
-                        nc.sync.dma_start(out=raw_pair[:, a, :], in_=byte_rows[kind][:, 2 * j + a, :])
-                else:
-                    nc.sync.dma_start(out=raw_pair[:], in_=byte_rows[kind][:, 2 * j : 2 * j + 2, :])
-                raw[kind, j] = raw_pair
-            for q, g in panels:
-                weights_panel = keep.tile([P, 2, 512], BF16, name=f"rho_{q}{g}")
-                nc.sync.dma_start(out=weights_panel[:], in_=rho_rows[:, 2 * q : 2 * q + 2, 512 * g : 512 * g + 512])
-                weights[q, g] = weights_panel
+
+        def load_pair(pair):
+            raw[pair] = keep.tile([P, 2, M], U8, name="raw_%s" % "".join(str(c) for c in pair))
+            rows = x_rows[pair[1]] if pair[0] == "x" else y_rows[pair[1], pair[2]]
+            nc.sync.dma_start(out=raw[pair][:], in_=rows)
+
+        def load_weights(q, g):
+            weights[q, g] = keep.tile([P, 2, 512], BF16, name=f"rho_{q}{g}")
+            nc.sync.dma_start(out=weights[q, g][:], in_=rho_rows[q][:, :, 512 * g : 512 * g + 512])
+
         h_codes = keep.tile([P, 4, 2 * R], U8, name="h_codes", align_bytes=64)
-        nc.sync.dma_start(out=h_codes[:].bitcast(I32), in_=h_words.rearrange("g p c -> p g c").bitcast(I32))
         h_plane = keep.tile([P, 4, R], U8, name="h_plane", align_bytes=64)
+        identity = keep.tile([P, P], F32, name="identity")
+        make_identity(nc, identity[:])
         nc.gpsimd.memset(h_plane[:].bitcast(I32), 0)
+
+        def pairs_at(s):
+            return [pair for pair in PAIRS if TURN_STEP[pair] == s]
+
+        def panels_at(s):
+            return [panel for panel in PANELS if PANEL_STEP[panel] == s]
+
+        for s in range(-2, LAST_STEP + 1):
+            for pair in pairs_at(s + 2):
+                load_pair(pair)
+            for panel in panels_at(s):
+                load_weights(*panel)
+        nc.sync.dma_start(out=h_codes[:].bitcast(I32), in_=h_words.rearrange("g p c -> p g c").bitcast(I32))
         for quad in range(4):
             nc.sync.dma_start(
                 out=h_plane[32 * quad : 32 * quad + 4, :, :].bitcast(I32),
                 in_=h_scales[:, 4 * quad : 4 * quad + 4, :].rearrange("g r n -> r g n").bitcast(I32),
             )
 
-        identity = keep.tile([P, P], F32, name="identity")
-        make_identity(nc, identity[:])
-
         codes = {}
         planes = {}
 
-        def operand(key, shape, name):
-            codes[key] = keep.tile(shape, U32, name=f"codes_{name}", align_bytes=64)
-            planes[key] = keep.tile(shape, U8, name=f"plane_{name}", align_bytes=64)
+        def operand(key, shape):
+            name = "".join(str(c) for c in key)
+            codes[key] = keep.tile(shape, U32, name="codes_" + name, align_bytes=64)
+            planes[key] = keep.tile(shape, U8, name="plane_" + name, align_bytes=64)
 
-        for g in range(4):
-            operand(("y", g), [P, 2, 512], f"y{g}")
+        for pair in PAIRS:
+            operand(pair, [P, 2, 256])
+        z_grouped = {}
         for q in range(4):
-            operand(("x", q), [P, 2, 256], f"x{q}")
-            for g in range(4):
-                operand(("z", q, g), [P, 256], f"z{q}{g}")
+            operand(("z", q), [P, 4, 256])
+            z_grouped[q] = keep.tile([P, 4, 2, P, 4], BF16, name=f"z_grouped{q}", align_bytes=64)
 
-        widened = {}
+        plain = {}
+        scaled = {}
         grouped = {}
+        pair_banks = {}
 
-        def widen(pair):
-            kind, j = pair
-            scale_tile = x_scales if kind == "x" else y_scales
-            widened[pair] = [wide_pool.tile([P, 2, 512], BF16, name="wide", align_bytes=64) for a in range(2)]
-            for engine in "vs":
+        def cast(pair):
+            if pair in CAST_FIRST:
+                plain[pair] = stage.tile([P, 2, M], BF16, name="plain", align_bytes=64)
+                nc.scalar.copy(out=plain[pair][:], in_=raw[pair][:].bitcast(FP8))
+
+        def scale(pair):
+            scaled[pair] = stage.tile([P, 2, 2, 2, 256], BF16, name="scaled", align_bytes=64)
+            by_block = scaled[pair][:].rearrange("r h w a (b j c) -> r h j a b w c", j=4, b=4)
+            if pair in CAST_FIRST:
+                source = plain[pair][:].rearrange("r a (h j b w c) -> r h j a b w c", h=2, j=4, b=4, w=2)
+                for h in range(2):
+                    for j in range(4):
+                        nc.vector.tensor_scalar(
+                            out=by_block[:, h, j],
+                            in0=source[:, h, j],
+                            scalar1=y_scales[:, pair[1], 4 * h + j : 4 * h + j + 1],
+                            scalar2=None,
+                            op0=MULT,
+                        )
+                return
+            for h in range(2):
                 for a in range(2):
-                    wide = widened[pair][a]
-                    for g in range(2):
-                        if WIDENED_BY[pair][a][g] != engine:
-                            continue
-                        for b in range(4):
-                            m0 = 512 * g + 128 * b
-                            values = raw[pair][:, a, m0 : m0 + 128].bitcast(FP8)
-                            scale = scale_tile[:, 2 * j + a, m0 // 128 : m0 // 128 + 1]
-                            if engine == "v":
-                                by_word = wide[:, g, :].rearrange("r (u p e) -> r p u e", u=2, e=2)
-                                nc.vector.tensor_scalar(
-                                    out=by_word[:, 32 * b : 32 * b + 32, :, :],
-                                    in0=values.rearrange("r (p u e) -> r p u e", u=2, e=2),
-                                    scalar1=scale,
-                                    scalar2=None,
-                                    op0=MULT,
-                                )
-                            else:
-                                nc.scalar.activation(out=wide[:, g, 128 * b : 128 * b + 128], in_=values, func=COPY, scale=scale)
+                    for j in range(4):
+                        m0 = 512 * h + 128 * j
+                        if pair[0] == "x":
+                            factor = x_scales[:, 2 * pair[1] + a, 4 * h + j : 4 * h + j + 1]
+                        else:
+                            factor = y_scales[:, pair[1], 4 * h + j : 4 * h + j + 1]
+                        nc.vector.tensor_scalar(
+                            out=by_block[:, h, j, a],
+                            in0=raw[pair][:, a, m0 : m0 + 128].bitcast(FP8).rearrange("r (b w c) -> r b w c", b=4, w=2),
+                            scalar1=factor,
+                            scalar2=None,
+                            op0=MULT,
+                        )
 
         def turn_pair(pair):
-            banks = []
-            for a in range(2):
+            words = scaled[pair][:].bitcast(F32)
+            pair_banks[pair] = []
+            for h in range(2):
                 bank = psum_turn.tile([P, 2, 2, P], F32, name="turn")
-                words = widened[pair][a][:].bitcast(F32)
-                for g in range(2):
-                    for u in range(2):
-                        if WIDENED_BY[pair][a][g] == "v":
-                            part = words[:, g, 128 * u : 128 * u + 128]
-                        else:
-                            part = words[:, g, u : 256 : 2]
-                        nc.tensor.transpose(bank[:, g, u, :], part, identity[:])
-                banks.append(bank)
-            return banks
+                for a in range(2):
+                    for w in range(2):
+                        nc.tensor.transpose(bank[:, a, w, :], words[:, h, w, a, :], identity[:])
+                pair_banks[pair].append(bank)
 
-        def empty_pair(pair, banks):
-            grouped[pair] = stage.tile([P, 2, 2, P, 4], BF16, name="grouped", align_bytes=64)
-            for a in range(2):
-                nc.scalar.copy(out=grouped[pair][:, :, a, :, :].bitcast(F32), in_=banks[a][:].rearrange("p g u r -> p g r u"))
+        def empty_pair(pair):
+            grouped[pair] = stage.tile([P, 2, 256, 4], BF16, name="grouped", align_bytes=64)
+            for h in range(2):
+                words = grouped[pair][:, h].bitcast(F32)
+                if pair[0] == "x":
+                    nc.scalar.copy(out=words.rearrange("p (a r) w -> p a r w", a=2), in_=pair_banks[pair][h][:].rearrange("p a w r -> p a r w"))
+                else:
+                    nc.scalar.copy(out=words.rearrange("p (r e) w -> p r e w", e=2), in_=pair_banks[pair][h][:].rearrange("p e w r -> p r e w"))
 
         def quantise_pair(pair):
-            kind, j = pair
-            if kind == "x":
-                nc.vector.quantize_mx(
-                    out=codes["x", j][:].rearrange("p g r -> p (g r)").bitcast(FP8X4),
-                    scales=planes["x", j][:].rearrange("p g r -> p (g r)"),
-                    in_=grouped[pair][:].rearrange("p g a r t -> p (g a r t)"),
-                )
-                return
-            rows = slice(256 * (j % 2), 256 * (j % 2) + 256)
-            for g in range(2):
-                nc.vector.quantize_mx(
-                    out=codes["y", j // 2][:, g, rows].bitcast(FP8X4),
-                    scales=planes["y", j // 2][:, g, rows],
-                    in_=grouped[pair][:, g, :, :, :].rearrange("p a r t -> p (a r t)"),
-                )
+            nc.vector.quantize_mx(
+                out=codes[pair][:].rearrange("p h r -> p (h r)").bitcast(FP8X4),
+                scales=planes[pair][:].rearrange("p h r -> p (h r)"),
+                in_=grouped[pair][:].rearrange("p h r t -> p (h r t)"),
+            )
 
-        def first_product(q, g):
-            banks = []
+        c_banks = {}
+        z_tiles = {}
+        z_banks = {}
+
+        def first_product(q, g, u):
+            acc = psum_acc.tile([P, 2, 256], F32, name="acc")
             for a in range(2):
-                acc = psum_acc.tile([P, 512], F32, name="acc")
                 rows = slice(128 * a, 128 * a + 128)
-                for k in range(2):
+                for h in range(2):
                     nc.tensor.matmul_mx(
-                        out=acc[:],
-                        lhsT=codes["x", q][:, k, rows].bitcast(FP8X4),
-                        lhsT_scale=planes["x", q][:, k, rows],
-                        rhs=codes["y", g][:, k, :].bitcast(FP8X4),
-                        rhs_scale=planes["y", g][:, k, :],
-                        start=(k == 0),
-                        stop=(k == 1),
+                        out=acc[:, a, :],
+                        lhsT=codes["x", q][:, h, rows].bitcast(FP8X4),
+                        lhsT_scale=planes["x", q][:, h, rows],
+                        rhs=codes["y", g, u][:, h, :].bitcast(FP8X4),
+                        rhs_scale=planes["y", g, u][:, h, :],
+                        start=(h == 0),
+                        stop=(h == 1),
                     )
-                banks.append(acc)
-            return banks
+            c_banks[q, g, u] = acc
 
-        def localise(q, g, banks):
-            tiles = []
-            for a in range(2):
-                z = stage.tile([P, 2, 256], BF16, name=f"z{a}", align_bytes=64)
-                for u in range(2):
-                    nc.vector.scalar_tensor_tensor(
-                        out=z[:, u, :].rearrange("r (p e) -> r p e", e=2),
-                        in0=banks[a][:].rearrange("r (p u e) -> r u p e", u=2, e=2)[:, u, :, :],
-                        scalar=1.0 / (M - 1),
-                        in1=weights[q, g][:, a, :].rearrange("r (p u e) -> r u p e", u=2, e=2)[:, u, :, :],
-                        op0=MULT,
-                        op1=MULT,
-                    )
-                tiles.append(z)
-            return tiles
+        def localise(q, g, u):
+            z = z_pool.tile([P, 2, 256], BF16, name=f"z{u}", align_bytes=64)
+            nc.vector.scalar_tensor_tensor(
+                out=z[:].rearrange("r a (p e) -> r (a p) e", e=2),
+                in0=c_banks[q, g, u][:].rearrange("r a (p e) -> r (a p) e", e=2),
+                scalar=1.0 / (M - 1),
+                in1=weights[q, g][:].rearrange("r a (p u e) -> r u (a p) e", u=2, e=2)[:, u],
+                op0=MULT,
+                op1=MULT,
+            )
+            z_tiles[q, g, u] = z
 
-        def turn_panel(tiles):
+        def turn_panel(q, g):
             bank = psum_turn.tile([P, 2, 2, P], F32, name="turn")
             for a in range(2):
-                words = tiles[a][:].bitcast(F32)
                 for u in range(2):
-                    nc.tensor.transpose(bank[:, a, u, :], words[:, u, :], identity[:])
-            return bank
+                    nc.tensor.transpose(bank[:, a, u, :], z_tiles[q, g, u][:].bitcast(F32)[:, a, :], identity[:])
+            z_banks[q, g] = bank
 
-        def empty_panel(bank):
-            z_grouped = stage.tile([P, 2, P, 4], BF16, name="z_grouped", align_bytes=64)
-            nc.scalar.copy(out=z_grouped[:].bitcast(F32), in_=bank[:].rearrange("p a u r -> p a r u"))
-            return z_grouped
+        def empty_panel(q, g):
+            nc.scalar.copy(out=z_grouped[q][:, g].bitcast(F32), in_=z_banks[q, g][:].rearrange("p a u r -> p a r u"))
 
-        def quantise_panel(q, g, z_grouped):
+        def quantise_z(q, g0, g1):
             nc.vector.quantize_mx(
-                out=codes["z", q, g][:].bitcast(FP8X4),
-                scales=planes["z", q, g][:],
-                in_=z_grouped[:].rearrange("p a r t -> p (a r t)"),
+                out=codes["z", q][:, g0:g1].rearrange("p g r -> p (g r)").bitcast(FP8X4),
+                scales=planes["z", q][:, g0:g1].rearrange("p g r -> p (g r)"),
+                in_=z_grouped[q][:, g0:g1].rearrange("p g a r t -> p (g a r t)"),
             )
 
-        def second_pass(i, g, acc, start, stop):
+        sums = {}
+
+        def second_product(i, g0, g1, pool=psum_acc, tag="acc"):
             q, a = divmod(i, 2)
             rows = slice(128 * a, 128 * a + 128)
-            nc.tensor.matmul_mx(
-                out=acc[:],
-                lhsT=codes["z", q, g][:, rows].bitcast(FP8X4),
-                lhsT_scale=planes["z", q, g][:, rows],
-                rhs=h_codes[:, g, :].bitcast(FP4X4),
-                rhs_scale=h_plane[:, g, :],
-                start=start,
-                stop=stop,
-            )
+            if g0 == 0:
+                sums[i] = pool.tile([P, R], F32, name=tag)
+            for g in range(g0, g1):
+                nc.tensor.matmul_mx(
+                    out=sums[i][:],
+                    lhsT=codes["z", q][:, g, rows].bitcast(FP8X4),
+                    lhsT_scale=planes["z", q][:, g, rows],
+                    rhs=h_codes[:, g, :].bitcast(FP4X4),
+                    rhs_scale=h_plane[:, g, :],
+                    start=(g == 0),
+                    stop=(g == 3),
+                )
 
-        def second_product(i):
-            acc = psum_acc.tile([P, R], F32, name="acc")
-            for g in range(4):
-                second_pass(i, g, acc, g == 0, g == 3)
-            return acc
-
-        def store(i, acc, on_vector=False):
+        def store(i, on_vector=False):
             rows = stage.tile([P, R], F32, name="out_rows")
             if on_vector:
-                nc.vector.tensor_copy(out=rows[:], in_=acc[:])
+                nc.vector.tensor_copy(out=rows[:], in_=sums[i][:])
             else:
-                nc.scalar.copy(out=rows[:], in_=acc[:])
-            nc.sync.dma_start(out=out[128 * i : 128 * i + 128, :], in_=rows[:])
+                nc.scalar.copy(out=rows[:], in_=sums[i][:])
+            nc.sync.dma_start(out=out_rows[i], in_=rows[:])
 
-        last_q = STEPS[-1][1][-1][0]
-        n_steps = len(STEPS)
-        steps = STEPS + [((), (), 2), ((), (), 8), ((), (), 8)]
-        turned_pairs = []
-        turned_panels = []
-        localised = []
-        panels_missing = [4, 4, 4, 4]
-        ready = []
-        summed = []
-        last_acc = []
-        last_panels = []
-        n_summed = 0
-        for pair in STEPS[0][0]:
-            widen(pair)
-        for s, (pairs, panels, n_out) in enumerate(steps):
-            for pair in steps[s + 1][0] if s + 1 < len(steps) else ():
-                widen(pair)
-            for pair in turned_pairs:
+        for s in range(-2, LAST_STEP + 1):
+            for pair in pairs_at(s + 2):
+                cast(pair)
+            for pair in pairs_at(s + 1):
+                scale(pair)
+            for panel in panels_at(s - 1):
+                localise(*panel, 0)
+                localise(*panel, 1)
+            for pair in pairs_at(s - 1):
                 quantise_pair(pair)
-            for q, g, z_grouped in turned_panels:
-                quantise_panel(q, g, z_grouped)
-                panels_missing[q] -= 1
-                if q == last_q:
-                    last_panels.append(g)
-                elif panels_missing[q] == 0:
-                    ready.extend([2 * q, 2 * q + 1])
+            if s == LAST_STEP - 1:
+                quantise_z(0, 0, 2)
+                quantise_z(1, 0, 2)
+            if s == LAST_STEP:
+                quantise_z(0, 2, 3)
+                quantise_z(1, 2, 3)
+            for pair in pairs_at(s):
+                turn_pair(pair)
+            for panel in panels_at(s - 2):
+                turn_panel(*panel)
+            for pair in pairs_at(s):
+                empty_pair(pair)
+            for panel in panels_at(s - 2):
+                empty_panel(*panel)
+            for panel in panels_at(s):
+                first_product(*panel, 0)
+                first_product(*panel, 1)
 
-            pair_banks = [turn_pair(pair) for pair in pairs]
-            due = [entry for entry in localised if entry[0] <= s - 2 or s >= n_steps]
-            if s >= n_steps:
-                due = due[:2]
-            localised = [entry for entry in localised if entry not in due]
-            panel_banks = [turn_panel(tiles) for made, q, g, tiles in due]
-            for pair, banks in zip(pairs, pair_banks):
-                empty_pair(pair, banks)
-            turned_pairs = pairs
-            turned_panels = [(q, g, empty_panel(bank)) for (made, q, g, tiles), bank in zip(due, panel_banks)]
-            for i, acc in summed:
-                store(i, acc)
-
-            products = [first_product(q, g) for q, g in panels]
-            summed = [(i, second_product(i)) for i in ready[:n_out]]
-            ready = ready[n_out:]
-            if s > n_steps and last_panels:
-                if not last_acc:
-                    for a in range(2):
-                        acc = psum_acc.tile([P, R], F32, name="acc")
-                        last_acc.append(acc)
-                for a in range(2):
-                    for n, g in enumerate(last_panels, n_summed):
-                        second_pass(2 * last_q + a, g, last_acc[a], n == 0, n == 3)
-                n_summed += len(last_panels)
-                last_panels = []
-                if n_summed == 4:
-                    summed.extend((2 * last_q + a, last_acc[a]) for a in range(2))
-            for (q, g), banks in zip(panels, products):
-                localised.append((s, q, g, localise(q, g, banks)))
-        for n, (i, acc) in enumerate(summed):
-            store(i, acc, on_vector=(n == 0))
+        for q in range(2):
+            turn_panel(q, 3)
+            empty_panel(q, 3)
+        for q in range(2, 4):
+            localise(q, 3, 0)
+            localise(q, 3, 1)
+            quantise_z(q - 2, 3, 4)
+        for i in range(2):
+            second_product(i, 0, 3, psum_turn, "turn")
+        for i in range(2):
+            second_product(i, 3, 4)
+        for q in range(2, 4):
+            quantise_z(q, 0, 2)
+            quantise_z(q, 2, 3)
+        for i in range(2):
+            store(i)
+        for q in range(2, 4):
+            turn_panel(q, 3)
+            empty_panel(q, 3)
+            quantise_z(q, 3, 4)
+        for i in range(2, 8):
+            second_product(i, 0, 4)
+            store(i, on_vector=(i % 2 == 1))

@@ -18,12 +18,28 @@ FP4X4 = mybir.dt.float4_e2m1fn_x4
 MULT = mybir.AluOpType.mult
 COPY = mybir.ActivationFunctionType.Copy
 
-PAIRS = [("x",0),("y", 0, 0), ("y", 0, 1),("x",1),("x",2),("x",3),("y", 1, 0), ("y", 1, 1),("y", 2, 0), ("y", 2, 1),("y", 3, 0), ("y", 3, 1)]
-TURN_STEP = dict(zip(PAIRS, [0,0,1,1,2,3,3,4,5,6,7,8]))
-PANELS = [(q,g) for g in range(4) for q in range(4)]
-PANEL_STEP = dict(zip(PANELS, [2,3,4,5,6,6,7,7,8,8,9,9,10,10,11,11]))
-LAST_STEP = max(PANEL_STEP.values())
+PAIRS = [("x",0),("x",1),("y", 0, 0), ("y", 0, 1),("x",2),("y", 1, 0), ("y", 1, 1),("x",3),("y", 2, 0), ("y", 2, 1),("y", 3, 0), ("y", 3, 1)]
+TURN_STEP = dict(zip(PAIRS, [0,0,1,1,2,3,4,5,6,7,8,9]))
+
+
+def spread_over_steps(earliest, per_step):
+    steps = {}
+    for item, s in earliest:
+        while list(steps.values()).count(s) == per_step:
+            s = s + 1
+        steps[item] = s
+    return steps
+
+
+UNIT_STEP = spread_over_steps(
+    [((q, g, u), max(TURN_STEP["x", q], TURN_STEP["y", g, u]) + 1) for g in range(4) for q in range(4) for u in range(2)], 4
+)
+UNITS = sorted(UNIT_STEP, key=UNIT_STEP.get)
+LAST_STEP = max(UNIT_STEP.values())
+PANELS = sorted(((q, g) for g in range(4) for q in range(4)), key=lambda panel: UNIT_STEP[panel + (1,)])
+PANEL_STEP = spread_over_steps([(panel, UNIT_STEP[panel + (1,)] + 2) for panel in PANELS], 2)
 CAST_FIRST = [p for p in PAIRS if p[0]=="y"]
+FIRST_LOADS = [("x",0),("y",0,0),("x",1),("y",0,1)]
 
 
 def tile_localised_ensemble_covariance_d4_kernel(tc, x_bytes, x_scale, y_bytes, y_scale, rho, h_words, h_scales, out):
@@ -38,11 +54,8 @@ def tile_localised_ensemble_covariance_d4_kernel(tc, x_bytes, x_scale, y_bytes, 
 
         x_scales = keep.tile([P, 8, 8], F32, name="x_scales")
         nc.scalar.dma_start(out=x_scales[:], in_=x_scale.rearrange("(p i) k -> p i k", p=P))
-        all_y_scales = keep.tile([P, 4, 4, 8], F32, name="all_y_scales")
-        nc.scalar.dma_start(out=all_y_scales[:].rearrange("p g quad k -> p (g quad k)"), in_=y_scale.rearrange("b k -> (b k)").partition_broadcast(P))
-        y_scales = keep.tile([P, 4, 8], F32, name="y_scales")
-        for quad in range(4):
-            nc.scalar.copy(out=y_scales[32 * quad : 32 * quad + 32, :, :], in_=all_y_scales[32 * quad : 32 * quad + 32, :, quad, :])
+        y_scale_column = keep.tile([P, 1], F32, name="y_scale_column")
+        nc.scalar.dma_start(out=y_scale_column[:], in_=y_scale.rearrange("b (k one) -> (b k) one", one=1))
 
         x_rows = x_bytes.rearrange("(p q a) k -> q p a k", a=2, p=P)
         y_rows = y_bytes.rearrange("(g p u e) k -> g u p e k", p=P, u=2, e=2)
@@ -63,20 +76,33 @@ def tile_localised_ensemble_covariance_d4_kernel(tc, x_bytes, x_scale, y_bytes, 
         h_codes = keep.tile([P, 4, 2 * R], U8, name="h_codes", align_bytes=64)
         h_plane = keep.tile([P, 4, R], U8, name="h_plane", align_bytes=64)
         identity = keep.tile([P, P], F32, name="identity")
-        make_identity(nc, identity[:])
-        nc.gpsimd.memset(h_plane[:].bitcast(I32), 0)
+        nc.vector.memset(identity[:], 0.0)
+        make_identity(nc, identity[:], nomemset=True)
+        nc.vector.memset(h_plane[:].bitcast(I32), 0)
+        spread = psum_acc.tile([P, 4, 4, 8], F32, name="acc")
+        nc.tensor.transpose(spread[:].rearrange("p g quad k -> p (g quad k)"), y_scale_column[:].to_broadcast([P, P]), identity[:])
+        y_scales = keep.tile([P, 4, 8], F32, name="y_scales")
+        for quad in range(4):
+            nc.scalar.copy(out=y_scales[32 * quad : 32 * quad + 32, :, :], in_=spread[32 * quad : 32 * quad + 32, :, quad, :])
 
         def pairs_at(s):
             return [pair for pair in PAIRS if TURN_STEP[pair] == s]
 
+        def units_at(s):
+            return [unit for unit in UNITS if UNIT_STEP[unit] == s]
+
         def panels_at(s):
             return [panel for panel in PANELS if PANEL_STEP[panel] == s]
 
+        for pair in FIRST_LOADS:
+            load_pair(pair)
         for s in range(-2, LAST_STEP + 1):
             for pair in pairs_at(s + 2):
-                load_pair(pair)
-            for panel in panels_at(s):
-                load_weights(*panel)
+                if pair not in raw:
+                    load_pair(pair)
+            for q, g, u in units_at(s):
+                if (q, g) not in weights:
+                    load_weights(q, g)
         nc.sync.dma_start(out=h_codes[:].bitcast(I32), in_=h_words.rearrange("g p c -> p g c").bitcast(I32))
         for quad in range(4):
             nc.sync.dma_start(
@@ -234,7 +260,7 @@ def tile_localised_ensemble_covariance_d4_kernel(tc, x_bytes, x_scale, y_bytes, 
                 )
 
         def store(i, on_vector=False):
-            rows = stage.tile([P, R], F32, name="out_rows")
+            rows = keep.tile([P, R], F32, name=f"out_rows{i}")
             if on_vector:
                 nc.vector.tensor_copy(out=rows[:], in_=sums[i][:])
             else:
@@ -242,53 +268,48 @@ def tile_localised_ensemble_covariance_d4_kernel(tc, x_bytes, x_scale, y_bytes, 
             nc.sync.dma_start(out=out_rows[i], in_=rows[:])
 
         for s in range(-2, LAST_STEP + 1):
-            for pair in pairs_at(s + 2):
-                cast(pair)
+            for unit in units_at(s - 1):
+                localise(*unit)
             for pair in pairs_at(s + 1):
                 scale(pair)
-            for panel in panels_at(s - 1):
-                localise(*panel, 0)
-                localise(*panel, 1)
-            for pair in pairs_at(s - 1):
-                quantise_pair(pair)
-            if s == LAST_STEP - 1:
-                quantise_z(0, 0, 2)
-                quantise_z(1, 0, 2)
-            if s == LAST_STEP:
-                quantise_z(0, 2, 3)
-                quantise_z(1, 2, 3)
             for pair in pairs_at(s):
                 turn_pair(pair)
-            for panel in panels_at(s - 2):
+            for panel in panels_at(s):
                 turn_panel(*panel)
             for pair in pairs_at(s):
                 empty_pair(pair)
-            for panel in panels_at(s - 2):
-                empty_panel(*panel)
             for panel in panels_at(s):
-                first_product(*panel, 0)
-                first_product(*panel, 1)
+                empty_panel(*panel)
+            for pair in pairs_at(s + 2):
+                cast(pair)
+            for unit in units_at(s):
+                first_product(*unit)
+            for pair in pairs_at(s):
+                quantise_pair(pair)
+            if s == LAST_STEP - 1:
+                quantise_z(0, 0, 2)
+            if s == LAST_STEP:
+                quantise_z(1, 0, 2)
+                quantise_z(0, 2, 3)
 
-        for q in range(2):
-            turn_panel(q, 3)
-            empty_panel(q, 3)
-        for q in range(2, 4):
-            localise(q, 3, 0)
-            localise(q, 3, 1)
-            quantise_z(q - 2, 3, 4)
+        for unit in units_at(LAST_STEP):
+            localise(*unit)
+        left = [panel for panel in PANELS if PANEL_STEP[panel] > LAST_STEP]
+        for panel in left[:-2]:
+            turn_panel(*panel)
+            empty_panel(*panel)
         for i in range(2):
-            second_product(i, 0, 3, psum_turn, "turn")
+            second_product(i, 0, 3)
+        quantise_z(0, 3, 4)
+        quantise_z(1, 2, 4)
+        for panel in left[-2:]:
+            turn_panel(*panel)
+            empty_panel(*panel)
         for i in range(2):
             second_product(i, 3, 4)
-        for q in range(2, 4):
-            quantise_z(q, 0, 2)
-            quantise_z(q, 2, 3)
-        for i in range(2):
             store(i)
         for q in range(2, 4):
-            turn_panel(q, 3)
-            empty_panel(q, 3)
-            quantise_z(q, 3, 4)
+            quantise_z(q, 0, 4)
         for i in range(2, 8):
             second_product(i, 0, 4)
-            store(i, on_vector=(i % 2 == 1))
+            store(i, on_vector=(i == 7))

@@ -18,8 +18,8 @@ FP4X4 = mybir.dt.float4_e2m1fn_x4
 MULT = mybir.AluOpType.mult
 COPY = mybir.ActivationFunctionType.Copy
 
-PAIRS = [("x",0),("x",1),("y", 0, 0), ("y", 0, 1),("x",2),("y", 1, 0), ("y", 1, 1),("x",3),("y", 2, 0), ("y", 2, 1),("y", 3, 0), ("y", 3, 1)]
-TURN_STEP = dict(zip(PAIRS, [0,0,1,1,2,3,4,5,6,7,8,9]))
+PAIRS = [("x",0),("y",0,0),("x",1),("y",0,1),("x",2),("y", 1, 0), ("y", 1, 1),("x",3),("y", 2, 0), ("y", 2, 1),("y", 3, 0), ("y", 3, 1)]
+TURN_STEP = dict(zip(PAIRS, [0,1,1,2,3,4,5,6,7,8,9,10]))
 
 
 def spread_over_steps(earliest, per_step):
@@ -39,7 +39,7 @@ LAST_STEP = max(UNIT_STEP.values())
 PANELS = sorted(((q, g) for g in range(4) for q in range(4)), key=lambda panel: UNIT_STEP[panel + (1,)])
 PANEL_STEP = spread_over_steps([(panel, UNIT_STEP[panel + (1,)] + 2) for panel in PANELS], 2)
 CAST_FIRST = [p for p in PAIRS if p[0]=="y"]
-FIRST_LOADS = [("x",0),("y",0,0),("x",1),("y",0,1)]
+FIRST_LOADS = []
 
 
 def tile_localised_ensemble_covariance_d4_kernel(tc, x_bytes, x_scale, y_bytes, y_scale, rho, h_words, h_scales, out):
@@ -64,10 +64,16 @@ def tile_localised_ensemble_covariance_d4_kernel(tc, x_bytes, x_scale, y_bytes, 
         raw = {}
         weights = {}
 
-        def load_pair(pair):
-            raw[pair] = keep.tile([P, 2, M], U8, name="raw_%s" % "".join(str(c) for c in pair))
+        def load_pair(pair, part=None):
+            if pair not in raw:
+                raw[pair] = keep.tile([P, 2, M], U8, name="raw_%s" % "".join(str(c) for c in pair))
             rows = x_rows[pair[1]] if pair[0] == "x" else y_rows[pair[1], pair[2]]
-            nc.sync.dma_start(out=raw[pair][:], in_=rows)
+            if part is None:
+                nc.sync.dma_start(out=raw[pair][:], in_=rows)
+            elif pair[0] == "x":
+                nc.sync.dma_start(out=raw[pair][:, :, 512 * part : 512 * part + 512], in_=rows[:, :, 512 * part : 512 * part + 512])
+            else:
+                nc.sync.dma_start(out=raw[pair][:, part, :], in_=rows[:, part, :])
 
         def load_weights(q, g):
             weights[q, g] = keep.tile([P, 2, 512], BF16, name=f"rho_{q}{g}")
@@ -94,10 +100,12 @@ def tile_localised_ensemble_covariance_d4_kernel(tc, x_bytes, x_scale, y_bytes, 
         def panels_at(s):
             return [panel for panel in PANELS if PANEL_STEP[panel] == s]
 
-        for pair in FIRST_LOADS:
-            load_pair(pair)
-        for s in range(-2, LAST_STEP + 1):
-            for pair in pairs_at(s + 2):
+        for n in range(2):
+            for part in range(2):
+                load_pair(("x", n), part)
+                load_pair(("y", 0, n), part)
+        for s in range(-3, LAST_STEP + 1):
+            for pair in pairs_at(s + 3):
                 if pair not in raw:
                     load_pair(pair)
             for q, g, u in units_at(s):
@@ -133,7 +141,11 @@ def tile_localised_ensemble_covariance_d4_kernel(tc, x_bytes, x_scale, y_bytes, 
         def cast(pair):
             if pair in CAST_FIRST:
                 plain[pair] = stage.tile([P, 2, M], BF16, name="plain", align_bytes=64)
-                nc.scalar.copy(out=plain[pair][:], in_=raw[pair][:].bitcast(FP8))
+                if pair[1] == 0:
+                    for a in range(2):
+                        nc.scalar.copy(out=plain[pair][:, a, :], in_=raw[pair][:, a, :].bitcast(FP8))
+                else:
+                    nc.scalar.copy(out=plain[pair][:], in_=raw[pair][:].bitcast(FP8))
 
         def scale(pair):
             scaled[pair] = stage.tile([P, 2, 2, 2, 256], BF16, name="scaled", align_bytes=64)
@@ -267,6 +279,30 @@ def tile_localised_ensemble_covariance_d4_kernel(tc, x_bytes, x_scale, y_bytes, 
                 nc.scalar.copy(out=rows[:], in_=sums[i][:])
             nc.sync.dma_start(out=out_rows[i], in_=rows[:])
 
+        def last_tile(i):
+            q, a = divmod(i, 2)
+            rows = slice(128 * a, 128 * a + 128)
+            width = R // 2
+            for part in range(2):
+                acc = psum_turn.tile([P, width], F32, name="turn")
+                for c0 in range(0, width, 128):
+                    for g in range(4):
+                        nc.tensor.matmul_mx(
+                            out=acc[:, c0 : c0 + 128],
+                            lhsT=codes["z", q][:, g, rows].bitcast(FP8X4),
+                            lhsT_scale=planes["z", q][:, g, rows],
+                            rhs=h_codes[:, g, 2 * (width * part + c0) : 2 * (width * part + c0 + 128)].bitcast(FP4X4),
+                            rhs_scale=h_plane[:, g, width * part + c0 : width * part + c0 + 128],
+                            start=(g == 0),
+                            stop=(g == 3),
+                        )
+                piece = keep.tile([P, width], F32, name=f"last_rows{part}")
+                if part % 2 == 0:
+                    nc.vector.tensor_copy(out=piece[:], in_=acc[:])
+                else:
+                    nc.scalar.copy(out=piece[:], in_=acc[:])
+                nc.sync.dma_start(out=out_rows[i][:, width * part : width * part + width], in_=piece[:])
+
         for s in range(-2, LAST_STEP + 1):
             for unit in units_at(s - 1):
                 localise(*unit)
@@ -310,6 +346,7 @@ def tile_localised_ensemble_covariance_d4_kernel(tc, x_bytes, x_scale, y_bytes, 
             store(i)
         for q in range(2, 4):
             quantise_z(q, 0, 4)
-        for i in range(2, 8):
+        for i in range(2, 7):
             second_product(i, 0, 4)
-            store(i, on_vector=(i == 7))
+            store(i)
+        last_tile(7)

@@ -40,6 +40,7 @@ PANELS = sorted(((q, g) for g in range(4) for q in range(4)), key=lambda panel: 
 PANEL_STEP = spread_over_steps([(panel, UNIT_STEP[panel + (1,)] + 2) for panel in PANELS], 2)
 CAST_FIRST = [p for p in PAIRS if p[0]=="y"]
 FIRST_LOADS = []
+CAST_BLOCKS = {p: (4, 6, 6, 6)[p[1]] for p in PAIRS if p[0] == "y"}
 
 
 def tile_localised_ensemble_covariance_d4_kernel(tc, x_bytes, x_scale, y_bytes, y_scale, rho, h_words, h_scales, out):
@@ -139,44 +140,39 @@ def tile_localised_ensemble_covariance_d4_kernel(tc, x_bytes, x_scale, y_bytes, 
         pair_banks = {}
 
         def cast(pair):
-            if pair in CAST_FIRST:
+            width = 128 * CAST_BLOCKS.get(pair, 0)
+            if width:
                 plain[pair] = stage.tile([P, 2, M], BF16, name="plain", align_bytes=64)
-                if pair[1] == 0:
-                    for a in range(2):
-                        nc.scalar.copy(out=plain[pair][:, a, :], in_=raw[pair][:, a, :].bitcast(FP8))
-                else:
-                    nc.scalar.copy(out=plain[pair][:], in_=raw[pair][:].bitcast(FP8))
+                for a in range(2):
+                    nc.scalar.copy(out=plain[pair][:, a, :width], in_=raw[pair][:, a, :width].bitcast(FP8))
 
         def scale(pair):
             scaled[pair] = stage.tile([P, 2, 2, 2, 256], BF16, name="scaled", align_bytes=64)
             by_block = scaled[pair][:].rearrange("r h w a (b j c) -> r h j a b w c", j=4, b=4)
-            if pair in CAST_FIRST:
-                source = plain[pair][:].rearrange("r a (h j b w c) -> r h j a b w c", h=2, j=4, b=4, w=2)
-                for h in range(2):
-                    for j in range(4):
-                        nc.vector.tensor_scalar(
-                            out=by_block[:, h, j],
-                            in0=source[:, h, j],
-                            scalar1=y_scales[:, pair[1], 4 * h + j : 4 * h + j + 1],
-                            scalar2=None,
-                            op0=MULT,
-                        )
-                return
-            for h in range(2):
+            for block in range(8):
+                h, j = divmod(block, 4)
+                members = slice(128 * block, 128 * block + 128)
+                if block < CAST_BLOCKS.get(pair, 0):
+                    nc.vector.tensor_scalar(
+                        out=by_block[:, h, j],
+                        in0=plain[pair][:, :, members].rearrange("r a (b w c) -> r a b w c", b=4, w=2),
+                        scalar1=y_scales[:, pair[1], block : block + 1],
+                        scalar2=None,
+                        op0=MULT,
+                    )
+                    continue
                 for a in range(2):
-                    for j in range(4):
-                        m0 = 512 * h + 128 * j
-                        if pair[0] == "x":
-                            factor = x_scales[:, 2 * pair[1] + a, 4 * h + j : 4 * h + j + 1]
-                        else:
-                            factor = y_scales[:, pair[1], 4 * h + j : 4 * h + j + 1]
-                        nc.vector.tensor_scalar(
-                            out=by_block[:, h, j, a],
-                            in0=raw[pair][:, a, m0 : m0 + 128].bitcast(FP8).rearrange("r (b w c) -> r b w c", b=4, w=2),
-                            scalar1=factor,
-                            scalar2=None,
-                            op0=MULT,
-                        )
+                    if pair[0] == "x":
+                        factor = x_scales[:, 2 * pair[1] + a, block : block + 1]
+                    else:
+                        factor = y_scales[:, pair[1], block : block + 1]
+                    nc.vector.tensor_scalar(
+                        out=by_block[:, h, j, a],
+                        in0=raw[pair][:, a, members].bitcast(FP8).rearrange("r (b w c) -> r b w c", b=4, w=2),
+                        scalar1=factor,
+                        scalar2=None,
+                        op0=MULT,
+                    )
 
         def turn_pair(pair):
             words = scaled[pair][:].bitcast(F32)
@@ -322,11 +318,8 @@ def tile_localised_ensemble_covariance_d4_kernel(tc, x_bytes, x_scale, y_bytes, 
                 first_product(*unit)
             for pair in pairs_at(s):
                 quantise_pair(pair)
-            if s == LAST_STEP - 1:
-                quantise_z(0, 0, 2)
             if s == LAST_STEP:
-                quantise_z(1, 0, 2)
-                quantise_z(0, 2, 3)
+                quantise_z(0, 0, 2)
 
         for unit in units_at(LAST_STEP):
             localise(*unit)
@@ -334,10 +327,11 @@ def tile_localised_ensemble_covariance_d4_kernel(tc, x_bytes, x_scale, y_bytes, 
         for panel in left[:-2]:
             turn_panel(*panel)
             empty_panel(*panel)
+        quantise_z(0, 2, 3)
         for i in range(2):
             second_product(i, 0, 3)
         quantise_z(0, 3, 4)
-        quantise_z(1, 2, 4)
+        quantise_z(1, 0, 4)
         for panel in left[-2:]:
             turn_panel(*panel)
             empty_panel(*panel)

@@ -40,7 +40,7 @@ PANELS = sorted(((q, g) for g in range(4) for q in range(4)), key=lambda panel: 
 PANEL_STEP = spread_over_steps([(panel, UNIT_STEP[panel + (1,)] + 2) for panel in PANELS], 2)
 CAST_FIRST = [p for p in PAIRS if p[0]=="y"]
 FIRST_LOADS = []
-CAST_BLOCKS = {p: (4, 6, 6, 6)[p[1]] for p in PAIRS if p[0] == "y"}
+CAST_BLOCKS = {p: (4, 8, 8, 8)[p[1]] for p in PAIRS if p[0] == "y"}
 
 
 def tile_localised_ensemble_covariance_d4_kernel(tc, x_bytes, x_scale, y_bytes, y_scale, rho, h_words, h_scales, out):
@@ -132,7 +132,8 @@ def tile_localised_ensemble_covariance_d4_kernel(tc, x_bytes, x_scale, y_bytes, 
         z_grouped = {}
         for q in range(4):
             operand(("z", q), [P, 4, 256])
-            z_grouped[q] = keep.tile([P, 4, 2, P, 4], BF16, name=f"z_grouped{q}", align_bytes=64)
+            for g in range(4):
+                z_grouped[q, g] = keep.tile([P, 2, P, 4], BF16, name=f"z_grouped{q}{g}", align_bytes=64)
 
         plain = {}
         scaled = {}
@@ -143,18 +144,21 @@ def tile_localised_ensemble_covariance_d4_kernel(tc, x_bytes, x_scale, y_bytes, 
             width = 128 * CAST_BLOCKS.get(pair, 0)
             if width:
                 plain[pair] = stage.tile([P, 2, M], BF16, name="plain", align_bytes=64)
-                for a in range(2):
-                    nc.scalar.copy(out=plain[pair][:, a, :width], in_=raw[pair][:, a, :width].bitcast(FP8))
+                if width == M:
+                    nc.scalar.copy(out=plain[pair][:], in_=raw[pair][:].bitcast(FP8))
+                else:
+                    for a in range(2):
+                        nc.scalar.copy(out=plain[pair][:, a, :width], in_=raw[pair][:, a, :width].bitcast(FP8))
 
         def scale(pair):
-            scaled[pair] = stage.tile([P, 2, 2, 2, 256], BF16, name="scaled", align_bytes=64)
-            by_block = scaled[pair][:].rearrange("r h w a (b j c) -> r h j a b w c", j=4, b=4)
+            scaled[pair] = [stage.tile([P, 2, 2, 256], BF16, name=f"scaled{h}", align_bytes=64) for h in range(2)]
+            by_block = [half[:].rearrange("r w a (b j c) -> r j a b w c", j=4, b=4) for half in scaled[pair]]
             for block in range(8):
                 h, j = divmod(block, 4)
                 members = slice(128 * block, 128 * block + 128)
                 if block < CAST_BLOCKS.get(pair, 0):
                     nc.vector.tensor_scalar(
-                        out=by_block[:, h, j],
+                        out=by_block[h][:, j],
                         in0=plain[pair][:, :, members].rearrange("r a (b w c) -> r a b w c", b=4, w=2),
                         scalar1=y_scales[:, pair[1], block : block + 1],
                         scalar2=None,
@@ -167,7 +171,7 @@ def tile_localised_ensemble_covariance_d4_kernel(tc, x_bytes, x_scale, y_bytes, 
                     else:
                         factor = y_scales[:, pair[1], block : block + 1]
                     nc.vector.tensor_scalar(
-                        out=by_block[:, h, j, a],
+                        out=by_block[h][:, j, a],
                         in0=raw[pair][:, a, members].bitcast(FP8).rearrange("r (b w c) -> r b w c", b=4, w=2),
                         scalar1=factor,
                         scalar2=None,
@@ -175,13 +179,13 @@ def tile_localised_ensemble_covariance_d4_kernel(tc, x_bytes, x_scale, y_bytes, 
                     )
 
         def turn_pair(pair):
-            words = scaled[pair][:].bitcast(F32)
             pair_banks[pair] = []
             for h in range(2):
+                words = scaled[pair][h][:].bitcast(F32)
                 bank = psum_turn.tile([P, 2, 2, P], F32, name="turn")
                 for a in range(2):
                     for w in range(2):
-                        nc.tensor.transpose(bank[:, a, w, :], words[:, h, w, a, :], identity[:])
+                        nc.tensor.transpose(bank[:, a, w, :], words[:, w, a, :], identity[:])
                 pair_banks[pair].append(bank)
 
         def empty_pair(pair):
@@ -240,14 +244,15 @@ def tile_localised_ensemble_covariance_d4_kernel(tc, x_bytes, x_scale, y_bytes, 
             z_banks[q, g] = bank
 
         def empty_panel(q, g):
-            nc.scalar.copy(out=z_grouped[q][:, g].bitcast(F32), in_=z_banks[q, g][:].rearrange("p a u r -> p a r u"))
+            nc.scalar.copy(out=z_grouped[q, g][:].bitcast(F32), in_=z_banks[q, g][:].rearrange("p a u r -> p a r u"))
 
         def quantise_z(q, g0, g1):
-            nc.vector.quantize_mx(
-                out=codes["z", q][:, g0:g1].rearrange("p g r -> p (g r)").bitcast(FP8X4),
-                scales=planes["z", q][:, g0:g1].rearrange("p g r -> p (g r)"),
-                in_=z_grouped[q][:, g0:g1].rearrange("p g a r t -> p (g a r t)"),
-            )
+            for g in range(g0, g1):
+                nc.vector.quantize_mx(
+                    out=codes["z", q][:, g].bitcast(FP8X4),
+                    scales=planes["z", q][:, g],
+                    in_=z_grouped[q, g][:].rearrange("p a r t -> p (a r t)"),
+                )
 
         sums = {}
 

@@ -16,31 +16,52 @@ FP8 = mybir.dt.float8_e4m3fn
 FP8X4 = mybir.dt.float8_e4m3fn_x4
 FP4X4 = mybir.dt.float4_e2m1fn_x4
 MULT = mybir.AluOpType.mult
-COPY = mybir.ActivationFunctionType.Copy
 
-PAIRS = [("x",0),("y",0,0),("x",1),("y",0,1),("x",2),("y", 1, 0), ("y", 1, 1),("x",3),("y", 2, 0), ("y", 2, 1),("y", 3, 0), ("y", 3, 1)]
-TURN_STEP = dict(zip(PAIRS, [0,1,1,2,3,4,5,6,7,8,9,10]))
+PAIRS = [("x", 0), ("y", 0, 0), ("x", 1), ("y", 0, 1), ("x", 2), ("y", 1, 0), ("y", 1, 1), ("x", 3)]
+PAIRS = PAIRS + [("y", g, u) for g in (2, 3) for u in range(2)]
+TURN_STEP = {pair: n if n < 2 else n - 1 for n, pair in enumerate(PAIRS)}
+BANKS_FOR_TRANSPOSES = 4
+BANKS_FOR_PRODUCTS = 4
+CAST_BLOCKS = {pair: 4 if pair[1] == 0 else 8 for pair in PAIRS if pair[0] == "y"}
+LOAD_AHEAD = 3
 
 
-def spread_over_steps(earliest, per_step):
+def spread_over_steps(earliest, room):
     steps = {}
-    for item, s in earliest:
-        while list(steps.values()).count(s) == per_step:
-            s = s + 1
-        steps[item] = s
+    for item, step in earliest:
+        while list(steps.values()).count(step) == room(step):
+            step = step + 1
+        steps[item] = step
     return steps
 
 
-UNIT_STEP = spread_over_steps(
-    [((q, g, u), max(TURN_STEP["x", q], TURN_STEP["y", g, u]) + 1) for g in range(4) for q in range(4) for u in range(2)], 4
+BANK_STEP = spread_over_steps(
+    [((q, g, u), max(TURN_STEP["x", q], TURN_STEP["y", g, u]) + 1) for g in range(4) for q in range(4) for u in range(2)],
+    lambda step: BANKS_FOR_PRODUCTS,
 )
-UNITS = sorted(UNIT_STEP, key=UNIT_STEP.get)
-LAST_STEP = max(UNIT_STEP.values())
-PANELS = sorted(((q, g) for g in range(4) for q in range(4)), key=lambda panel: UNIT_STEP[panel + (1,)])
-PANEL_STEP = spread_over_steps([(panel, UNIT_STEP[panel + (1,)] + 2) for panel in PANELS], 2)
-CAST_FIRST = [p for p in PAIRS if p[0]=="y"]
-FIRST_LOADS = []
-CAST_BLOCKS = {p: (4, 8, 8, 8)[p[1]] for p in PAIRS if p[0] == "y"}
+BANKS = sorted(BANK_STEP, key=BANK_STEP.get)
+LAST_STEP = max(BANK_STEP.values())
+PANELS = sorted(((q, g) for g in range(4) for q in range(4)), key=lambda panel: BANK_STEP[panel + (1,)])
+PANEL_STEP = spread_over_steps(
+    [(panel, BANK_STEP[panel + (1,)] + 2) for panel in PANELS],
+    lambda step: BANKS_FOR_TRANSPOSES - (2 if step in TURN_STEP.values() else 0),
+)
+
+
+def pairs_at(step):
+    return [pair for pair in PAIRS if TURN_STEP[pair] == step]
+
+
+def banks_at(step):
+    return [bank for bank in BANKS if BANK_STEP[bank] == step]
+
+
+def panels_at(step):
+    return [panel for panel in PANELS if PANEL_STEP[panel] == step]
+
+
+def label(key):
+    return "".join(str(part) for part in key)
 
 
 def tile_localised_ensemble_covariance_d4_kernel(tc, x_bytes, x_scale, y_bytes, y_scale, rho, h_words, h_scales, out):
@@ -49,36 +70,14 @@ def tile_localised_ensemble_covariance_d4_kernel(tc, x_bytes, x_scale, y_bytes, 
         keep = ctx.enter_context(tc.tile_pool(name="keep", bufs=1))
         stage = ctx.enter_context(tc.tile_pool(name="stage", bufs=3))
         z_pool = ctx.enter_context(tc.tile_pool(name="z_pool", bufs=6))
-        psum_turn = ctx.enter_context(tc.psum_pool(name="psum_turn", bufs=4))
-        psum_acc = ctx.enter_context(tc.psum_pool(name="psum_acc", bufs=4))
+        psum_turn = ctx.enter_context(tc.psum_pool(name="psum_turn", bufs=BANKS_FOR_TRANSPOSES))
+        psum_acc = ctx.enter_context(tc.psum_pool(name="psum_acc", bufs=BANKS_FOR_PRODUCTS))
         ctx.enter_context(tc.manual_schedule())
 
         x_scales = keep.tile([P, 8, 8], F32, name="x_scales")
         nc.scalar.dma_start(out=x_scales[:], in_=x_scale.rearrange("(p i) k -> p i k", p=P))
         y_scale_column = keep.tile([P, 1], F32, name="y_scale_column")
         nc.scalar.dma_start(out=y_scale_column[:], in_=y_scale.rearrange("b (k one) -> (b k) one", one=1))
-
-        x_rows = x_bytes.rearrange("(p q a) k -> q p a k", a=2, p=P)
-        y_rows = y_bytes.rearrange("(g p u e) k -> g u p e k", p=P, u=2, e=2)
-        rho_rows = rho.rearrange("(p q a) n -> q p a n", a=2, p=P)
-        out_rows = out.rearrange("(p i) r -> i p r", p=P)
-        raw = {}
-        weights = {}
-
-        def load_pair(pair, part=None):
-            if pair not in raw:
-                raw[pair] = keep.tile([P, 2, M], U8, name="raw_%s" % "".join(str(c) for c in pair))
-            rows = x_rows[pair[1]] if pair[0] == "x" else y_rows[pair[1], pair[2]]
-            if part is None:
-                nc.sync.dma_start(out=raw[pair][:], in_=rows)
-            elif pair[0] == "x":
-                nc.sync.dma_start(out=raw[pair][:, :, 512 * part : 512 * part + 512], in_=rows[:, :, 512 * part : 512 * part + 512])
-            else:
-                nc.sync.dma_start(out=raw[pair][:, part, :], in_=rows[:, part, :])
-
-        def load_weights(q, g):
-            weights[q, g] = keep.tile([P, 2, 512], BF16, name=f"rho_{q}{g}")
-            nc.sync.dma_start(out=weights[q, g][:], in_=rho_rows[q][:, :, 512 * g : 512 * g + 512])
 
         h_codes = keep.tile([P, 4, 2 * R], U8, name="h_codes", align_bytes=64)
         h_plane = keep.tile([P, 4, R], U8, name="h_plane", align_bytes=64)
@@ -92,24 +91,31 @@ def tile_localised_ensemble_covariance_d4_kernel(tc, x_bytes, x_scale, y_bytes, 
         for quad in range(4):
             nc.scalar.copy(out=y_scales[32 * quad : 32 * quad + 32, :, :], in_=spread[32 * quad : 32 * quad + 32, :, quad, :])
 
-        def pairs_at(s):
-            return [pair for pair in PAIRS if TURN_STEP[pair] == s]
+        x_rows = x_bytes.rearrange("(p q a) k -> q p a k", a=2, p=P)
+        y_rows = y_bytes.rearrange("(g p u e) k -> g u p e k", p=P, u=2, e=2)
+        rho_rows = rho.rearrange("(p q a) n -> q p a n", a=2, p=P)
+        out_rows = out.rearrange("(p i) r -> i p r", p=P)
+        raw = {}
+        weights = {}
 
-        def units_at(s):
-            return [unit for unit in UNITS if UNIT_STEP[unit] == s]
+        def load_pair(pair, members=slice(0, M)):
+            if pair not in raw:
+                raw[pair] = keep.tile([P, 2, M], U8, name="raw_" + label(pair))
+            rows = x_rows[pair[1]] if pair[0] == "x" else y_rows[pair[1], pair[2]]
+            nc.sync.dma_start(out=raw[pair][:, :, members], in_=rows[:, :, members])
 
-        def panels_at(s):
-            return [panel for panel in PANELS if PANEL_STEP[panel] == s]
+        def load_weights(q, g):
+            weights[q, g] = keep.tile([P, 2, 512], BF16, name=f"rho_{q}{g}")
+            nc.sync.dma_start(out=weights[q, g][:], in_=rho_rows[q][:, :, 512 * g : 512 * g + 512])
 
-        for n in range(2):
-            for part in range(2):
-                load_pair(("x", n), part)
-                load_pair(("y", 0, n), part)
-        for s in range(-3, LAST_STEP + 1):
-            for pair in pairs_at(s + 3):
+        for h in range(2):
+            for pair in PAIRS[:2]:
+                load_pair(pair, slice(512 * h, 512 * h + 512))
+        for step in range(-LOAD_AHEAD, LAST_STEP + 1):
+            for pair in pairs_at(step + LOAD_AHEAD):
                 if pair not in raw:
                     load_pair(pair)
-            for q, g, u in units_at(s):
+            for q, g, u in banks_at(step):
                 if (q, g) not in weights:
                     load_weights(q, g)
         nc.sync.dma_start(out=h_codes[:].bitcast(I32), in_=h_words.rearrange("g p c -> p g c").bitcast(I32))
@@ -123,9 +129,8 @@ def tile_localised_ensemble_covariance_d4_kernel(tc, x_bytes, x_scale, y_bytes, 
         planes = {}
 
         def operand(key, shape):
-            name = "".join(str(c) for c in key)
-            codes[key] = keep.tile(shape, U32, name="codes_" + name, align_bytes=64)
-            planes[key] = keep.tile(shape, U8, name="plane_" + name, align_bytes=64)
+            codes[key] = keep.tile(shape, U32, name="codes_" + label(key), align_bytes=64)
+            planes[key] = keep.tile(shape, U8, name="plane_" + label(key), align_bytes=64)
 
         for pair in PAIRS:
             operand(pair, [P, 2, 256])
@@ -137,12 +142,12 @@ def tile_localised_ensemble_covariance_d4_kernel(tc, x_bytes, x_scale, y_bytes, 
 
         plain = {}
         scaled = {}
-        grouped = {}
         pair_banks = {}
+        grouped = {}
 
         def cast(pair):
-            width = 128 * CAST_BLOCKS.get(pair, 0)
-            if width:
+            if pair[0] == "y":
+                width = 128 * CAST_BLOCKS[pair]
                 plain[pair] = stage.tile([P, 2, M], BF16, name="plain", align_bytes=64)
                 if width == M:
                     nc.scalar.copy(out=plain[pair][:], in_=raw[pair][:].bitcast(FP8))
@@ -246,8 +251,8 @@ def tile_localised_ensemble_covariance_d4_kernel(tc, x_bytes, x_scale, y_bytes, 
         def empty_panel(q, g):
             nc.scalar.copy(out=z_grouped[q, g][:].bitcast(F32), in_=z_banks[q, g][:].rearrange("p a u r -> p a r u"))
 
-        def quantise_z(q, g0, g1):
-            for g in range(g0, g1):
+        def quantise_z(q, groups):
+            for g in groups:
                 nc.vector.quantize_mx(
                     out=codes["z", q][:, g].bitcast(FP8X4),
                     scales=planes["z", q][:, g],
@@ -256,96 +261,86 @@ def tile_localised_ensemble_covariance_d4_kernel(tc, x_bytes, x_scale, y_bytes, 
 
         sums = {}
 
-        def second_product(i, g0, g1, pool=psum_acc, tag="acc"):
+        def second_pass(acc, i, g, first, width):
             q, a = divmod(i, 2)
             rows = slice(128 * a, 128 * a + 128)
-            if g0 == 0:
-                sums[i] = pool.tile([P, R], F32, name=tag)
-            for g in range(g0, g1):
-                nc.tensor.matmul_mx(
-                    out=sums[i][:],
-                    lhsT=codes["z", q][:, g, rows].bitcast(FP8X4),
-                    lhsT_scale=planes["z", q][:, g, rows],
-                    rhs=h_codes[:, g, :].bitcast(FP4X4),
-                    rhs_scale=h_plane[:, g, :],
-                    start=(g == 0),
-                    stop=(g == 3),
-                )
+            nc.tensor.matmul_mx(
+                out=acc,
+                lhsT=codes["z", q][:, g, rows].bitcast(FP8X4),
+                lhsT_scale=planes["z", q][:, g, rows],
+                rhs=h_codes[:, g, 2 * first : 2 * (first + width)].bitcast(FP4X4),
+                rhs_scale=h_plane[:, g, first : first + width],
+                start=(g == 0),
+                stop=(g == 3),
+            )
 
-        def store(i, on_vector=False):
+        def second_product(i, groups):
+            if i not in sums:
+                sums[i] = psum_acc.tile([P, R], F32, name="acc")
+            for g in groups:
+                second_pass(sums[i][:], i, g, 0, R)
+
+        def store(i):
             rows = keep.tile([P, R], F32, name=f"out_rows{i}")
-            if on_vector:
-                nc.vector.tensor_copy(out=rows[:], in_=sums[i][:])
-            else:
-                nc.scalar.copy(out=rows[:], in_=sums[i][:])
+            nc.scalar.copy(out=rows[:], in_=sums[i][:])
             nc.sync.dma_start(out=out_rows[i], in_=rows[:])
 
         def last_tile(i):
-            q, a = divmod(i, 2)
-            rows = slice(128 * a, 128 * a + 128)
-            width = R // 2
-            for part in range(2):
-                acc = psum_turn.tile([P, width], F32, name="turn")
-                for c0 in range(0, width, 128):
+            for side in range(2):
+                acc = psum_turn.tile([P, 256], F32, name="turn")
+                for first in range(0, 256, 128):
                     for g in range(4):
-                        nc.tensor.matmul_mx(
-                            out=acc[:, c0 : c0 + 128],
-                            lhsT=codes["z", q][:, g, rows].bitcast(FP8X4),
-                            lhsT_scale=planes["z", q][:, g, rows],
-                            rhs=h_codes[:, g, 2 * (width * part + c0) : 2 * (width * part + c0 + 128)].bitcast(FP4X4),
-                            rhs_scale=h_plane[:, g, width * part + c0 : width * part + c0 + 128],
-                            start=(g == 0),
-                            stop=(g == 3),
-                        )
-                piece = keep.tile([P, width], F32, name=f"last_rows{part}")
-                if part % 2 == 0:
-                    nc.vector.tensor_copy(out=piece[:], in_=acc[:])
+                        second_pass(acc[:, first : first + 128], i, g, 256 * side + first, 128)
+                columns = keep.tile([P, 256], F32, name=f"last_columns{side}")
+                if side == 0:
+                    nc.vector.tensor_copy(out=columns[:], in_=acc[:])
                 else:
-                    nc.scalar.copy(out=piece[:], in_=acc[:])
-                nc.sync.dma_start(out=out_rows[i][:, width * part : width * part + width], in_=piece[:])
+                    nc.scalar.copy(out=columns[:], in_=acc[:])
+                nc.sync.dma_start(out=out_rows[i][:, 256 * side : 256 * side + 256], in_=columns[:])
 
-        for s in range(-2, LAST_STEP + 1):
-            for unit in units_at(s - 1):
-                localise(*unit)
-            for pair in pairs_at(s + 1):
+        for step in range(-2, LAST_STEP + 1):
+            for bank in banks_at(step - 1):
+                localise(*bank)
+            for pair in pairs_at(step + 1):
                 scale(pair)
-            for pair in pairs_at(s):
+            for pair in pairs_at(step):
                 turn_pair(pair)
-            for panel in panels_at(s):
+            for panel in panels_at(step):
                 turn_panel(*panel)
-            for pair in pairs_at(s):
+            for pair in pairs_at(step):
                 empty_pair(pair)
-            for panel in panels_at(s):
+            for panel in panels_at(step):
                 empty_panel(*panel)
-            for pair in pairs_at(s + 2):
+            for pair in pairs_at(step + 2):
                 cast(pair)
-            for unit in units_at(s):
-                first_product(*unit)
-            for pair in pairs_at(s):
+            for bank in banks_at(step):
+                first_product(*bank)
+            for pair in pairs_at(step):
                 quantise_pair(pair)
-            if s == LAST_STEP:
-                quantise_z(0, 0, 2)
 
-        for unit in units_at(LAST_STEP):
-            localise(*unit)
-        left = [panel for panel in PANELS if PANEL_STEP[panel] > LAST_STEP]
-        for panel in left[:-2]:
-            turn_panel(*panel)
-            empty_panel(*panel)
-        quantise_z(0, 2, 3)
-        for i in range(2):
-            second_product(i, 0, 3)
-        quantise_z(0, 3, 4)
-        quantise_z(1, 0, 4)
-        for panel in left[-2:]:
-            turn_panel(*panel)
-            empty_panel(*panel)
-        for i in range(2):
-            second_product(i, 3, 4)
+        quantise_z(0, (0, 1))
+        for bank in banks_at(LAST_STEP):
+            localise(*bank)
+        for i in (0, 1):
+            second_product(i, (0, 1))
+        quantise_z(0, (2,))
+        quantise_z(1, (0, 1, 2))
+        for q in range(4):
+            turn_panel(q, 3)
+            empty_panel(q, 3)
+        for i in (2, 3):
+            second_product(i, (0, 1))
+        quantise_z(0, (3,))
+        for i in (0, 1):
+            second_product(i, (2, 3))
             store(i)
-        for q in range(2, 4):
-            quantise_z(q, 0, 4)
-        for i in range(2, 7):
-            second_product(i, 0, 4)
+        quantise_z(1, (3,))
+        quantise_z(2, range(4))
+        for i in (2, 3):
+            second_product(i, (2, 3))
+            store(i)
+        quantise_z(3, range(4))
+        for i in (4, 5, 6):
+            second_product(i, range(4))
             store(i)
         last_tile(7)

@@ -76,8 +76,6 @@ def tile_localised_ensemble_covariance_d4_kernel(tc, x_bytes, x_scale, y_bytes, 
 
         x_scales = keep.tile([P, 8, 8], F32, name="x_scales")
         nc.scalar.dma_start(out=x_scales[:], in_=x_scale.rearrange("(p i) k -> p i k", p=P))
-        y_scale_column = keep.tile([P, 1], F32, name="y_scale_column")
-        nc.scalar.dma_start(out=y_scale_column[:], in_=y_scale.rearrange("b (k one) -> (b k) one", one=1))
 
         h_codes = keep.tile([P, 4, 2 * R], U8, name="h_codes", align_bytes=64)
         h_plane = keep.tile([P, 4, R], U8, name="h_plane", align_bytes=64)
@@ -85,11 +83,6 @@ def tile_localised_ensemble_covariance_d4_kernel(tc, x_bytes, x_scale, y_bytes, 
         nc.vector.memset(identity[:], 0.0)
         make_identity(nc, identity[:], nomemset=True)
         nc.vector.memset(h_plane[:].bitcast(I32), 0)
-        spread = psum_acc.tile([P, 4, 4, 8], F32, name="acc")
-        nc.tensor.transpose(spread[:].rearrange("p g quad k -> p (g quad k)"), y_scale_column[:].to_broadcast([P, P]), identity[:])
-        y_scales = keep.tile([P, 4, 8], F32, name="y_scales")
-        for quad in range(4):
-            nc.scalar.copy(out=y_scales[32 * quad : 32 * quad + 32, :, :], in_=spread[32 * quad : 32 * quad + 32, :, quad, :])
 
         x_rows = x_bytes.rearrange("(p q a) k -> q p a k", a=2, p=P)
         y_rows = y_bytes.rearrange("(g p u e) k -> g u p e k", p=P, u=2, e=2)
@@ -108,9 +101,12 @@ def tile_localised_ensemble_covariance_d4_kernel(tc, x_bytes, x_scale, y_bytes, 
             weights[q, g] = keep.tile([P, 2, 512], BF16, name=f"rho_{q}{g}")
             nc.sync.dma_start(out=weights[q, g][:], in_=rho_rows[q][:, :, 512 * g : 512 * g + 512])
 
-        for h in range(2):
-            for pair in PAIRS[:2]:
-                load_pair(pair, slice(512 * h, 512 * h + 512))
+        for pair in PAIRS[:2]:
+            load_pair(pair, slice(0, 512))
+        y_scale_column = keep.tile([P, 1], F32, name="y_scale_column")
+        nc.sync.dma_start(out=y_scale_column[:], in_=y_scale.rearrange("b (k one) -> (b k) one", one=1))
+        for pair in PAIRS[:2]:
+            load_pair(pair, slice(512, M))
         for step in range(-LOAD_AHEAD, LAST_STEP + 1):
             for pair in pairs_at(step + LOAD_AHEAD):
                 if pair not in raw:
@@ -124,6 +120,7 @@ def tile_localised_ensemble_covariance_d4_kernel(tc, x_bytes, x_scale, y_bytes, 
                 out=h_plane[32 * quad : 32 * quad + 4, :, :].bitcast(I32),
                 in_=h_scales[:, 4 * quad : 4 * quad + 4, :].rearrange("g r n -> r g n").bitcast(I32),
             )
+
 
         codes = {}
         planes = {}
@@ -298,7 +295,14 @@ def tile_localised_ensemble_covariance_d4_kernel(tc, x_bytes, x_scale, y_bytes, 
                     nc.scalar.copy(out=columns[:], in_=acc[:])
                 nc.sync.dma_start(out=out_rows[i][:, 256 * side : 256 * side + 256], in_=columns[:])
 
-        for step in range(-2, LAST_STEP + 1):
+        scale(PAIRS[0])
+        cast(PAIRS[1])
+        spread = psum_acc.tile([P, 4, 4, 8], F32, name="acc")
+        nc.tensor.transpose(spread[:].rearrange("p g quad k -> p (g quad k)"), y_scale_column[:].to_broadcast([P, P]), identity[:])
+        y_scales = keep.tile([P, 4, 8], F32, name="y_scales")
+        for quad in range(4):
+            nc.scalar.copy(out=y_scales[32 * quad : 32 * quad + 32, :, :], in_=spread[32 * quad : 32 * quad + 32, :, quad, :])
+        for step in range(LAST_STEP + 1):
             for bank in banks_at(step - 1):
                 localise(*bank)
             for pair in pairs_at(step + 1):

@@ -191,20 +191,21 @@ def tile_localised_ensemble_covariance_d4_kernel(tc, x_bytes, x_scale, y_bytes, 
                 pair_banks[pair].append(bank)
 
         def empty_pair(pair):
-            grouped[pair] = stage.tile([P, 2, 256, 4], BF16, name="grouped", align_bytes=64)
+            grouped[pair] = [stage.tile([P, 256, 4], BF16, name=f"grouped{h}", align_bytes=64) for h in range(2)]
             for h in range(2):
-                words = grouped[pair][:, h].bitcast(F32)
+                words = grouped[pair][h][:].bitcast(F32)
                 if pair[0] == "x":
                     nc.scalar.copy(out=words.rearrange("p (a r) w -> p a r w", a=2), in_=pair_banks[pair][h][:].rearrange("p a w r -> p a r w"))
                 else:
                     nc.scalar.copy(out=words.rearrange("p (r e) w -> p r e w", e=2), in_=pair_banks[pair][h][:].rearrange("p e w r -> p r e w"))
 
         def quantise_pair(pair):
-            nc.vector.quantize_mx(
-                out=codes[pair][:].rearrange("p h r -> p (h r)").bitcast(FP8X4),
-                scales=planes[pair][:].rearrange("p h r -> p (h r)"),
-                in_=grouped[pair][:].rearrange("p h r t -> p (h r t)"),
-            )
+            for h in range(2):
+                nc.vector.quantize_mx(
+                    out=codes[pair][:, h].bitcast(FP8X4),
+                    scales=planes[pair][:, h],
+                    in_=grouped[pair][h][:].rearrange("p r t -> p (r t)"),
+                )
 
         c_banks = {}
         z_tiles = {}
@@ -289,7 +290,7 @@ def tile_localised_ensemble_covariance_d4_kernel(tc, x_bytes, x_scale, y_bytes, 
                     for g in range(4):
                         second_pass(acc[:, first : first + 128], i, g, 256 * side + first, 128)
                 columns = keep.tile([P, 256], F32, name=f"last_columns{side}")
-                if side == 0:
+                if side == 1:
                     nc.vector.tensor_copy(out=columns[:], in_=acc[:])
                 else:
                     nc.scalar.copy(out=columns[:], in_=acc[:])

@@ -121,7 +121,6 @@ def tile_localised_ensemble_covariance_d4_kernel(tc, x_bytes, x_scale, y_bytes, 
                 in_=h_scales[:, 4 * quad : 4 * quad + 4, :].rearrange("g r n -> r g n").bitcast(I32),
             )
 
-
         codes = {}
         planes = {}
 
@@ -155,30 +154,28 @@ def tile_localised_ensemble_covariance_d4_kernel(tc, x_bytes, x_scale, y_bytes, 
         def scale(pair):
             scaled[pair] = [stage.tile([P, 2, 2, 256], BF16, name=f"scaled{h}", align_bytes=64) for h in range(2)]
             by_block = [half[:].rearrange("r w a (b j c) -> r j a b w c", j=4, b=4) for half in scaled[pair]]
-            for block in range(8):
+            cast_blocks = CAST_BLOCKS.get(pair, 0)
+            for block in range(cast_blocks):
                 h, j = divmod(block, 4)
-                members = slice(128 * block, 128 * block + 128)
-                if block < CAST_BLOCKS.get(pair, 0):
-                    nc.vector.tensor_scalar(
-                        out=by_block[h][:, j],
-                        in0=plain[pair][:, :, members].rearrange("r a (b w c) -> r a b w c", b=4, w=2),
-                        scalar1=y_scales[:, pair[1], block : block + 1],
-                        scalar2=None,
-                        op0=MULT,
-                    )
-                    continue
+                nc.vector.tensor_scalar(
+                    out=by_block[h][:, j],
+                    in0=plain[pair][:, :, 128 * block : 128 * block + 128].rearrange("r a (b w c) -> r a b w c", b=4, w=2),
+                    scalar1=y_scales[:, pair[1], block : block + 1],
+                    scalar2=None,
+                    op0=MULT,
+                )
+            for h in range(cast_blocks // 4, 2):
                 for a in range(2):
-                    if pair[0] == "x":
-                        factor = x_scales[:, 2 * pair[1] + a, block : block + 1]
-                    else:
-                        factor = y_scales[:, pair[1], block : block + 1]
-                    nc.vector.tensor_scalar(
-                        out=by_block[h][:, j, a],
-                        in0=raw[pair][:, a, members].bitcast(FP8).rearrange("r (b w c) -> r b w c", b=4, w=2),
-                        scalar1=factor,
-                        scalar2=None,
-                        op0=MULT,
-                    )
+                    factors = x_scales[:, 2 * pair[1] + a] if pair[0] == "x" else y_scales[:, pair[1]]
+                    for j in range(4):
+                        block = 4 * h + j
+                        nc.vector.tensor_scalar(
+                            out=by_block[h][:, j, a],
+                            in0=raw[pair][:, a, 128 * block : 128 * block + 128].bitcast(FP8).rearrange("r (b w c) -> r b w c", b=4, w=2),
+                            scalar1=factors[:, block : block + 1],
+                            scalar2=None,
+                            op0=MULT,
+                        )
 
         def turn_pair(pair):
             pair_banks[pair] = []
@@ -213,17 +210,17 @@ def tile_localised_ensemble_covariance_d4_kernel(tc, x_bytes, x_scale, y_bytes, 
 
         def first_product(q, g, u):
             acc = psum_acc.tile([P, 2, 256], F32, name="acc")
-            for a in range(2):
-                rows = slice(128 * a, 128 * a + 128)
-                for h in range(2):
+            for h in range(2):
+                for a in range(2):
+                    rows = slice(128 * a, 128 * a + 128)
                     nc.tensor.matmul_mx(
                         out=acc[:, a, :],
                         lhsT=codes["x", q][:, h, rows].bitcast(FP8X4),
                         lhsT_scale=planes["x", q][:, h, rows],
                         rhs=codes["y", g, u][:, h, :].bitcast(FP8X4),
                         rhs_scale=planes["y", g, u][:, h, :],
-                        start=(h == 0),
-                        stop=(h == 1),
+                        start=(h == 0 and a == 0),
+                        stop=(h == 1 and a == 1),
                     )
             c_banks[q, g, u] = acc
 
@@ -290,10 +287,10 @@ def tile_localised_ensemble_covariance_d4_kernel(tc, x_bytes, x_scale, y_bytes, 
                     for g in range(4):
                         second_pass(acc[:, first : first + 128], i, g, 256 * side + first, 128)
                 columns = keep.tile([P, 256], F32, name=f"last_columns{side}")
-                if side == 1:
-                    nc.vector.tensor_copy(out=columns[:], in_=acc[:])
-                else:
+                if side == 0:
                     nc.scalar.copy(out=columns[:], in_=acc[:])
+                else:
+                    nc.vector.tensor_copy(out=columns[:], in_=acc[:])
                 nc.sync.dma_start(out=out_rows[i][:, 256 * side : 256 * side + 256], in_=columns[:])
 
         scale(PAIRS[0])
@@ -303,6 +300,7 @@ def tile_localised_ensemble_covariance_d4_kernel(tc, x_bytes, x_scale, y_bytes, 
         y_scales = keep.tile([P, 4, 8], F32, name="y_scales")
         for quad in range(4):
             nc.scalar.copy(out=y_scales[32 * quad : 32 * quad + 32, :, :], in_=spread[32 * quad : 32 * quad + 32, :, quad, :])
+
         for step in range(LAST_STEP + 1):
             for bank in banks_at(step - 1):
                 localise(*bank)

@@ -22,7 +22,7 @@ PAIRS = PAIRS + [("y", g, u) for g in (2, 3) for u in range(2)]
 TURN_STEP = {pair: n if n < 2 else n - 1 for n, pair in enumerate(PAIRS)}
 BANKS_FOR_TRANSPOSES = 4
 BANKS_FOR_PRODUCTS = 4
-CAST_BLOCKS = {pair: 4 if pair[1] == 0 else 8 for pair in PAIRS if pair[0] == "y"}
+CAST_HALVES = {pair: 1 if pair[1] == 0 else 2 for pair in PAIRS if pair[0] == "y"}
 LOAD_AHEAD = 3
 
 
@@ -35,15 +35,15 @@ def spread_over_steps(earliest, room):
     return steps
 
 
-BANK_STEP = spread_over_steps(
+PRODUCT_STEP = spread_over_steps(
     [((q, g, u), max(TURN_STEP["x", q], TURN_STEP["y", g, u]) + 1) for g in range(4) for q in range(4) for u in range(2)],
     lambda step: BANKS_FOR_PRODUCTS,
 )
-BANKS = sorted(BANK_STEP, key=BANK_STEP.get)
-LAST_STEP = max(BANK_STEP.values())
-PANELS = sorted(((q, g) for g in range(4) for q in range(4)), key=lambda panel: BANK_STEP[panel + (1,)])
+PRODUCTS = sorted(PRODUCT_STEP, key=PRODUCT_STEP.get)
+LAST_STEP = max(PRODUCT_STEP.values())
+PANELS = sorted(((q, g) for g in range(4) for q in range(4)), key=lambda panel: PRODUCT_STEP[panel + (1,)])
 PANEL_STEP = spread_over_steps(
-    [(panel, BANK_STEP[panel + (1,)] + 2) for panel in PANELS],
+    [(panel, PRODUCT_STEP[panel + (1,)] + 2) for panel in PANELS],
     lambda step: BANKS_FOR_TRANSPOSES - (2 if step in TURN_STEP.values() else 0),
 )
 
@@ -52,8 +52,15 @@ def pairs_at(step):
     return [pair for pair in PAIRS if TURN_STEP[pair] == step]
 
 
-def banks_at(step):
-    return [bank for bank in BANKS if BANK_STEP[bank] == step]
+def halves_at(step):
+    halves = [(pair, half) for pair in pairs_at(step) for half in range(2)]
+    if len(halves) == 4:
+        return [halves[2], halves[0], halves[1], halves[3]]
+    return halves
+
+
+def products_at(step):
+    return [product for product in PRODUCTS if PRODUCT_STEP[product] == step]
 
 
 def panels_at(step):
@@ -97,21 +104,26 @@ def tile_localised_ensemble_covariance_d4_kernel(tc, x_bytes, x_scale, y_bytes, 
             rows = x_rows[pair[1]] if pair[0] == "x" else y_rows[pair[1], pair[2]]
             nc.sync.dma_start(out=raw[pair][:, :, members], in_=rows[:, :, members])
 
+        def load_half(pair, half):
+            load_pair(pair, slice(512 * half, 512 * half + 512))
+
         def load_weights(q, g):
             weights[q, g] = keep.tile([P, 2, 512], BF16, name=f"rho_{q}{g}")
             nc.sync.dma_start(out=weights[q, g][:], in_=rho_rows[q][:, :, 512 * g : 512 * g + 512])
 
-        for pair in PAIRS[:2]:
-            load_pair(pair, slice(0, 512))
+        load_half(("x", 0), 0)
+        load_half(("y", 0, 0), 0)
         y_scale_column = keep.tile([P, 1], F32, name="y_scale_column")
         nc.sync.dma_start(out=y_scale_column[:], in_=y_scale.rearrange("b (k one) -> (b k) one", one=1))
-        for pair in PAIRS[:2]:
-            load_pair(pair, slice(512, M))
+        load_half(("x", 0), 1)
+        load_half(("x", 1), 0)
+        load_half(("y", 0, 0), 1)
+        load_half(("x", 1), 1)
         for step in range(-LOAD_AHEAD, LAST_STEP + 1):
             for pair in pairs_at(step + LOAD_AHEAD):
                 if pair not in raw:
                     load_pair(pair)
-            for q, g, u in banks_at(step):
+            for q, g, u in products_at(step):
                 if (q, g) not in weights:
                     load_weights(q, g)
         nc.sync.dma_start(out=h_codes[:].bitcast(I32), in_=h_words.rearrange("g p c -> p g c").bitcast(I32))
@@ -138,71 +150,68 @@ def tile_localised_ensemble_covariance_d4_kernel(tc, x_bytes, x_scale, y_bytes, 
 
         plain = {}
         scaled = {}
-        pair_banks = {}
+        half_banks = {}
         grouped = {}
 
         def cast(pair):
             if pair[0] == "y":
-                width = 128 * CAST_BLOCKS[pair]
+                width = 512 * CAST_HALVES[pair]
                 plain[pair] = stage.tile([P, 2, M], BF16, name="plain", align_bytes=64)
                 if width == M:
                     nc.scalar.copy(out=plain[pair][:], in_=raw[pair][:].bitcast(FP8))
                 else:
-                    for a in range(2):
-                        nc.scalar.copy(out=plain[pair][:, a, :width], in_=raw[pair][:, a, :width].bitcast(FP8))
+                    for e in range(2):
+                        nc.scalar.copy(out=plain[pair][:, e, :width], in_=raw[pair][:, e, :width].bitcast(FP8))
 
-        def scale(pair):
-            scaled[pair] = [stage.tile([P, 2, 2, 256], BF16, name=f"scaled{h}", align_bytes=64) for h in range(2)]
-            by_block = [half[:].rearrange("r w a (b j c) -> r j a b w c", j=4, b=4) for half in scaled[pair]]
-            cast_blocks = CAST_BLOCKS.get(pair, 0)
-            for block in range(cast_blocks):
-                h, j = divmod(block, 4)
-                nc.vector.tensor_scalar(
-                    out=by_block[h][:, j],
-                    in0=plain[pair][:, :, 128 * block : 128 * block + 128].rearrange("r a (b w c) -> r a b w c", b=4, w=2),
-                    scalar1=y_scales[:, pair[1], block : block + 1],
-                    scalar2=None,
-                    op0=MULT,
-                )
-            for h in range(cast_blocks // 4, 2):
-                for a in range(2):
-                    factors = x_scales[:, 2 * pair[1] + a] if pair[0] == "x" else y_scales[:, pair[1]]
-                    for j in range(4):
-                        block = 4 * h + j
-                        nc.vector.tensor_scalar(
-                            out=by_block[h][:, j, a],
-                            in0=raw[pair][:, a, 128 * block : 128 * block + 128].bitcast(FP8).rearrange("r (b w c) -> r b w c", b=4, w=2),
-                            scalar1=factors[:, block : block + 1],
-                            scalar2=None,
-                            op0=MULT,
-                        )
+        def scale(pair, half):
+            scaled[pair, half] = stage.tile([P, 2, 2, 256], BF16, name=f"scaled{half}", align_bytes=64)
+            by_span = scaled[pair, half][:].rearrange("r w tile (b j c) -> r j tile b w c", j=4, b=4)
+            if half < CAST_HALVES.get(pair, 0):
+                for j in range(4):
+                    span = 4 * half + j
+                    nc.vector.tensor_scalar(
+                        out=by_span[:, j],
+                        in0=plain[pair][:, :, 128 * span : 128 * span + 128].rearrange("r tile (b w c) -> r tile b w c", b=4, w=2),
+                        scalar1=y_scales[:, pair[1], span : span + 1],
+                        scalar2=None,
+                        op0=MULT,
+                    )
+                return
+            for tile in range(2):
+                factors = x_scales[:, 2 * pair[1] + tile] if pair[0] == "x" else y_scales[:, pair[1]]
+                for j in range(4):
+                    span = 4 * half + j
+                    nc.vector.tensor_scalar(
+                        out=by_span[:, j, tile],
+                        in0=raw[pair][:, tile, 128 * span : 128 * span + 128].bitcast(FP8).rearrange("r (b w c) -> r b w c", b=4, w=2),
+                        scalar1=factors[:, span : span + 1],
+                        scalar2=None,
+                        op0=MULT,
+                    )
 
-        def turn_pair(pair):
-            pair_banks[pair] = []
-            for h in range(2):
-                words = scaled[pair][h][:].bitcast(F32)
-                bank = psum_turn.tile([P, 2, 2, P], F32, name="turn")
-                for a in range(2):
-                    for w in range(2):
-                        nc.tensor.transpose(bank[:, a, w, :], words[:, w, a, :], identity[:])
-                pair_banks[pair].append(bank)
+        def turn_half(pair, half):
+            words = scaled[pair, half][:].bitcast(F32)
+            bank = psum_turn.tile([P, 2, 2, P], F32, name="turn")
+            for tile in range(2):
+                for w in range(2):
+                    nc.tensor.transpose(bank[:, tile, w, :], words[:, w, tile, :], identity[:])
+            half_banks[pair, half] = bank
 
-        def empty_pair(pair):
-            grouped[pair] = [stage.tile([P, 256, 4], BF16, name=f"grouped{h}", align_bytes=64) for h in range(2)]
-            for h in range(2):
-                words = grouped[pair][h][:].bitcast(F32)
-                if pair[0] == "x":
-                    nc.scalar.copy(out=words.rearrange("p (a r) w -> p a r w", a=2), in_=pair_banks[pair][h][:].rearrange("p a w r -> p a r w"))
-                else:
-                    nc.scalar.copy(out=words.rearrange("p (r e) w -> p r e w", e=2), in_=pair_banks[pair][h][:].rearrange("p e w r -> p r e w"))
+        def empty_half(pair, half):
+            grouped[pair, half] = stage.tile([P, 256, 4], BF16, name=f"grouped{half}", align_bytes=64)
+            words = grouped[pair, half][:].bitcast(F32)
+            bank = half_banks[pair, half]
+            if pair[0] == "x":
+                nc.scalar.copy(out=words.rearrange("p (a r) w -> p a r w", a=2), in_=bank[:].rearrange("p a w r -> p a r w"))
+            else:
+                nc.scalar.copy(out=words.rearrange("p (r e) w -> p r e w", e=2), in_=bank[:].rearrange("p e w r -> p r e w"))
 
-        def quantise_pair(pair):
-            for h in range(2):
-                nc.vector.quantize_mx(
-                    out=codes[pair][:, h].bitcast(FP8X4),
-                    scales=planes[pair][:, h],
-                    in_=grouped[pair][h][:].rearrange("p r t -> p (r t)"),
-                )
+        def quantise_half(pair, half):
+            nc.vector.quantize_mx(
+                out=codes[pair][:, half].bitcast(FP8X4),
+                scales=planes[pair][:, half],
+                in_=grouped[pair, half][:].rearrange("p r t -> p (r t)"),
+            )
 
         c_banks = {}
         z_tiles = {}
@@ -210,17 +219,17 @@ def tile_localised_ensemble_covariance_d4_kernel(tc, x_bytes, x_scale, y_bytes, 
 
         def first_product(q, g, u):
             acc = psum_acc.tile([P, 2, 256], F32, name="acc")
-            for h in range(2):
-                for a in range(2):
-                    rows = slice(128 * a, 128 * a + 128)
+            for a in range(2):
+                rows = slice(128 * a, 128 * a + 128)
+                for half in range(2):
                     nc.tensor.matmul_mx(
                         out=acc[:, a, :],
-                        lhsT=codes["x", q][:, h, rows].bitcast(FP8X4),
-                        lhsT_scale=planes["x", q][:, h, rows],
-                        rhs=codes["y", g, u][:, h, :].bitcast(FP8X4),
-                        rhs_scale=planes["y", g, u][:, h, :],
-                        start=(h == 0 and a == 0),
-                        stop=(h == 1 and a == 1),
+                        lhsT=codes["x", q][:, half, rows].bitcast(FP8X4),
+                        lhsT_scale=planes["x", q][:, half, rows],
+                        rhs=codes["y", g, u][:, half, :].bitcast(FP8X4),
+                        rhs_scale=planes["y", g, u][:, half, :],
+                        start=(half == 0),
+                        stop=(half == 1),
                     )
             c_banks[q, g, u] = acc
 
@@ -293,8 +302,9 @@ def tile_localised_ensemble_covariance_d4_kernel(tc, x_bytes, x_scale, y_bytes, 
                     nc.vector.tensor_copy(out=columns[:], in_=acc[:])
                 nc.sync.dma_start(out=out_rows[i][:, 256 * side : 256 * side + 256], in_=columns[:])
 
-        scale(PAIRS[0])
-        cast(PAIRS[1])
+        for pair, half in halves_at(0):
+            scale(pair, half)
+        cast(("y", 0, 0))
         spread = psum_acc.tile([P, 4, 4, 8], F32, name="acc")
         nc.tensor.transpose(spread[:].rearrange("p g quad k -> p (g quad k)"), y_scale_column[:].to_broadcast([P, P]), identity[:])
         y_scales = keep.tile([P, 4, 8], F32, name="y_scales")
@@ -302,28 +312,28 @@ def tile_localised_ensemble_covariance_d4_kernel(tc, x_bytes, x_scale, y_bytes, 
             nc.scalar.copy(out=y_scales[32 * quad : 32 * quad + 32, :, :], in_=spread[32 * quad : 32 * quad + 32, :, quad, :])
 
         for step in range(LAST_STEP + 1):
-            for bank in banks_at(step - 1):
-                localise(*bank)
-            for pair in pairs_at(step + 1):
-                scale(pair)
-            for pair in pairs_at(step):
-                turn_pair(pair)
+            for product in products_at(step - 1):
+                localise(*product)
+            for pair, half in halves_at(step + 1):
+                scale(pair, half)
+            for pair, half in halves_at(step):
+                turn_half(pair, half)
             for panel in panels_at(step):
                 turn_panel(*panel)
-            for pair in pairs_at(step):
-                empty_pair(pair)
+            for pair, half in halves_at(step):
+                empty_half(pair, half)
             for panel in panels_at(step):
                 empty_panel(*panel)
             for pair in pairs_at(step + 2):
                 cast(pair)
-            for bank in banks_at(step):
-                first_product(*bank)
-            for pair in pairs_at(step):
-                quantise_pair(pair)
+            for product in products_at(step):
+                first_product(*product)
+            for pair, half in halves_at(step):
+                quantise_half(pair, half)
 
         quantise_z(0, (0, 1))
-        for bank in banks_at(LAST_STEP):
-            localise(*bank)
+        for product in products_at(LAST_STEP):
+            localise(*product)
         for i in (0, 1):
             second_product(i, (0, 1))
         quantise_z(0, (2,))

@@ -20,6 +20,7 @@ MULT = mybir.AluOpType.mult
 PAIRS = [("x", 0), ("y", 0, 0), ("x", 1), ("y", 0, 1), ("x", 2), ("y", 1, 0), ("y", 1, 1), ("x", 3)]
 PAIRS = PAIRS + [("y", g, u) for g in (2, 3) for u in range(2)]
 TURN_STEP = {pair: n if n < 2 else n - 1 for n, pair in enumerate(PAIRS)}
+BANKS = 8
 BANKS_FOR_TRANSPOSES = 4
 BANKS_FOR_PRODUCTS = 4
 CAST_HALVES = {pair: 1 if pair[1] == 0 else 2 for pair in PAIRS if pair[0] == "y"}
@@ -64,7 +65,7 @@ def products_at(step):
 
 
 def panels_at(step):
-    return [panel for panel in PANELS if PANEL_STEP[panel] == step]
+    return [panel for panel in PANELS if PANEL_STEP[panel] == step and step < LAST_STEP]
 
 
 def label(key):
@@ -76,9 +77,8 @@ def tile_localised_ensemble_covariance_d4_kernel(tc, x_bytes, x_scale, y_bytes, 
     with ExitStack() as ctx:
         keep = ctx.enter_context(tc.tile_pool(name="keep", bufs=1))
         stage = ctx.enter_context(tc.tile_pool(name="stage", bufs=3))
-        z_pool = ctx.enter_context(tc.tile_pool(name="z_pool", bufs=6))
-        psum_turn = ctx.enter_context(tc.psum_pool(name="psum_turn", bufs=BANKS_FOR_TRANSPOSES))
-        psum_acc = ctx.enter_context(tc.psum_pool(name="psum_acc", bufs=BANKS_FOR_PRODUCTS))
+        z_pool = ctx.enter_context(tc.tile_pool(name="z_pool", bufs=8))
+        psum = ctx.enter_context(tc.psum_pool(name="psum", bufs=BANKS))
         ctx.enter_context(tc.manual_schedule())
 
         x_scales = keep.tile([P, 8, 8], F32, name="x_scales")
@@ -112,10 +112,10 @@ def tile_localised_ensemble_covariance_d4_kernel(tc, x_bytes, x_scale, y_bytes, 
             nc.sync.dma_start(out=weights[q, g][:], in_=rho_rows[q][:, :, 512 * g : 512 * g + 512])
 
         load_half(("x", 0), 0)
+        load_half(("x", 0), 1)
         load_half(("y", 0, 0), 0)
         y_scale_column = keep.tile([P, 1], F32, name="y_scale_column")
         nc.sync.dma_start(out=y_scale_column[:], in_=y_scale.rearrange("b (k one) -> (b k) one", one=1))
-        load_half(("x", 0), 1)
         load_half(("x", 1), 0)
         load_half(("y", 0, 0), 1)
         load_half(("x", 1), 1)
@@ -191,7 +191,7 @@ def tile_localised_ensemble_covariance_d4_kernel(tc, x_bytes, x_scale, y_bytes, 
 
         def turn_half(pair, half):
             words = scaled[pair, half][:].bitcast(F32)
-            bank = psum_turn.tile([P, 2, 2, P], F32, name="turn")
+            bank = psum.tile([P, 2, 2, P], F32, name="bank")
             for tile in range(2):
                 for w in range(2):
                     nc.tensor.transpose(bank[:, tile, w, :], words[:, w, tile, :], identity[:])
@@ -218,7 +218,7 @@ def tile_localised_ensemble_covariance_d4_kernel(tc, x_bytes, x_scale, y_bytes, 
         z_banks = {}
 
         def first_product(q, g, u):
-            acc = psum_acc.tile([P, 2, 256], F32, name="acc")
+            acc = psum.tile([P, 2, 256], F32, name="bank")
             for a in range(2):
                 rows = slice(128 * a, 128 * a + 128)
                 for half in range(2):
@@ -246,7 +246,7 @@ def tile_localised_ensemble_covariance_d4_kernel(tc, x_bytes, x_scale, y_bytes, 
             z_tiles[q, g, u] = z
 
         def turn_panel(q, g):
-            bank = psum_turn.tile([P, 2, 2, P], F32, name="turn")
+            bank = psum.tile([P, 2, 2, P], F32, name="bank")
             for a in range(2):
                 for u in range(2):
                     nc.tensor.transpose(bank[:, a, u, :], z_tiles[q, g, u][:].bitcast(F32)[:, a, :], identity[:])
@@ -280,7 +280,7 @@ def tile_localised_ensemble_covariance_d4_kernel(tc, x_bytes, x_scale, y_bytes, 
 
         def second_product(i, groups):
             if i not in sums:
-                sums[i] = psum_acc.tile([P, R], F32, name="acc")
+                sums[i] = psum.tile([P, R], F32, name="bank")
             for g in groups:
                 second_pass(sums[i][:], i, g, 0, R)
 
@@ -291,10 +291,9 @@ def tile_localised_ensemble_covariance_d4_kernel(tc, x_bytes, x_scale, y_bytes, 
 
         def last_tile(i):
             for side in range(2):
-                acc = psum_turn.tile([P, 256], F32, name="turn")
-                for first in range(0, 256, 128):
-                    for g in range(4):
-                        second_pass(acc[:, first : first + 128], i, g, 256 * side + first, 128)
+                acc = psum.tile([P, 256], F32, name="bank")
+                for g in range(4):
+                    second_pass(acc[:], i, g, 256 * side, 256)
                 columns = keep.tile([P, 256], F32, name=f"last_columns{side}")
                 if side == 0:
                     nc.scalar.copy(out=columns[:], in_=acc[:])
@@ -305,7 +304,7 @@ def tile_localised_ensemble_covariance_d4_kernel(tc, x_bytes, x_scale, y_bytes, 
         for pair, half in halves_at(0):
             scale(pair, half)
         cast(("y", 0, 0))
-        spread = psum_acc.tile([P, 4, 4, 8], F32, name="acc")
+        spread = psum.tile([P, 4, 4, 8], F32, name="bank")
         nc.tensor.transpose(spread[:].rearrange("p g quad k -> p (g quad k)"), y_scale_column[:].to_broadcast([P, P]), identity[:])
         y_scales = keep.tile([P, 4, 8], F32, name="y_scales")
         for quad in range(4):
@@ -331,29 +330,17 @@ def tile_localised_ensemble_covariance_d4_kernel(tc, x_bytes, x_scale, y_bytes, 
             for pair, half in halves_at(step):
                 quantise_half(pair, half)
 
-        quantise_z(0, (0, 1))
         for product in products_at(LAST_STEP):
             localise(*product)
-        for i in (0, 1):
-            second_product(i, (0, 1))
-        quantise_z(0, (2,))
-        quantise_z(1, (0, 1, 2))
+        quantise_z(0, (0, 1))
         for q in range(4):
-            turn_panel(q, 3)
-            empty_panel(q, 3)
-        for i in (2, 3):
-            second_product(i, (0, 1))
-        quantise_z(0, (3,))
-        for i in (0, 1):
-            second_product(i, (2, 3))
-            store(i)
-        quantise_z(1, (3,))
-        quantise_z(2, range(4))
-        for i in (2, 3):
-            second_product(i, (2, 3))
-            store(i)
-        quantise_z(3, range(4))
-        for i in (4, 5, 6):
+            for g in (2, 3):
+                turn_panel(q, g)
+                empty_panel(q, g)
+        quantise_z(0, (2, 3))
+        for q in (1, 2, 3):
+            quantise_z(q, range(4))
+        for i in range(7):
             second_product(i, range(4))
             store(i)
         last_tile(7)

@@ -86,6 +86,15 @@ def tile_localised_ensemble_covariance_d4_kernel(tc, x_bytes, x_scale, y_bytes, 
 
         h_codes = keep.tile([P, 4, 2 * R], U8, name="h_codes", align_bytes=64)
         h_plane = keep.tile([P, 4, R], U8, name="h_plane", align_bytes=64)
+        zeros = keep.tile([P, 320], F32, name="zeros")
+        nc.vector.memset(zeros[:], 0.0)
+        warm = psum.tile([P, 320], F32, name="bank")
+
+        def warm_up(columns):
+            nc.tensor.matmul(warm[:, :columns], lhsT=zeros[:, :P], rhs=zeros[:, :columns], start=True, stop=True)
+
+        for repeat in range(2):
+            warm_up(320)
         identity = keep.tile([P, P], F32, name="identity")
         nc.vector.memset(identity[:], 0.0)
         make_identity(nc, identity[:], nomemset=True)
@@ -315,8 +324,10 @@ def tile_localised_ensemble_covariance_d4_kernel(tc, x_bytes, x_scale, y_bytes, 
                 localise(*product)
             for pair, half in halves_at(step + 1):
                 scale(pair, half)
-            for pair, half in halves_at(step):
+            for n, (pair, half) in enumerate(halves_at(step)):
                 turn_half(pair, half)
+                if step < 2 and n % 2 == 1:
+                    warm_up(192)
             for panel in panels_at(step):
                 turn_panel(*panel)
             for pair, half in halves_at(step):

@@ -24,6 +24,7 @@ BANKS = 8
 BANKS_FOR_TRANSPOSES = 4
 BANKS_FOR_PRODUCTS = 4
 CAST_HALVES = {pair: 1 if pair[1] == 0 else 2 for pair in PAIRS if pair[0] == "y"}
+SCALAR_HALF = (("x", 3), 1)
 LOAD_AHEAD = 3
 
 
@@ -121,10 +122,10 @@ def tile_localised_ensemble_covariance_d4_kernel(tc, x_bytes, x_scale, y_bytes, 
             nc.sync.dma_start(out=weights[q, g][:], in_=rho_rows[q][:, :, 512 * g : 512 * g + 512])
 
         load_half(("x", 0), 0)
-        load_half(("x", 0), 1)
         load_half(("y", 0, 0), 0)
         y_scale_column = keep.tile([P, 1], F32, name="y_scale_column")
         nc.sync.dma_start(out=y_scale_column[:], in_=y_scale.rearrange("b (k one) -> (b k) one", one=1))
+        load_half(("x", 0), 1)
         load_half(("x", 1), 0)
         load_half(("y", 0, 0), 1)
         load_half(("x", 1), 1)
@@ -158,11 +159,14 @@ def tile_localised_ensemble_covariance_d4_kernel(tc, x_bytes, x_scale, y_bytes, 
                 z_grouped[q, g] = keep.tile([P, 2, P, 4], BF16, name=f"z_grouped{q}{g}", align_bytes=64)
 
         plain = {}
+        in_order = {}
         scaled = {}
         half_banks = {}
         grouped = {}
 
         def cast(pair):
+            if pair == SCALAR_HALF[0]:
+                widen_on_scalar(*SCALAR_HALF)
             if pair[0] == "y":
                 width = 512 * CAST_HALVES[pair]
                 plain[pair] = stage.tile([P, 2, M], BF16, name="plain", align_bytes=64)
@@ -175,6 +179,13 @@ def tile_localised_ensemble_covariance_d4_kernel(tc, x_bytes, x_scale, y_bytes, 
         def scale(pair, half):
             scaled[pair, half] = stage.tile([P, 2, 2, 256], BF16, name=f"scaled{half}", align_bytes=64)
             by_span = scaled[pair, half][:].rearrange("r w tile (b j c) -> r j tile b w c", j=4, b=4)
+            if (pair, half) in in_order:
+                for tile in range(2):
+                    nc.vector.tensor_copy(
+                        out=by_span[:, :, tile],
+                        in_=in_order[pair, half][:, tile].rearrange("r (j b w c) -> r j b w c", j=4, b=4, w=2),
+                    )
+                return
             if half < CAST_HALVES.get(pair, 0):
                 for j in range(4):
                     span = 4 * half + j
@@ -196,6 +207,18 @@ def tile_localised_ensemble_covariance_d4_kernel(tc, x_bytes, x_scale, y_bytes, 
                         scalar1=factors[:, span : span + 1],
                         scalar2=None,
                         op0=MULT,
+                    )
+
+        def widen_on_scalar(pair, half):
+            in_order[pair, half] = keep.tile([P, 2, 512], BF16, name="in_order", align_bytes=64)
+            for tile in range(2):
+                for j in range(4):
+                    span = 4 * half + j
+                    nc.scalar.activation(
+                        out=in_order[pair, half][:, tile, 128 * j : 128 * j + 128],
+                        in_=raw[pair][:, tile, 128 * span : 128 * span + 128].bitcast(FP8),
+                        func=mybir.ActivationFunctionType.Copy,
+                        scale=x_scales[:, 2 * pair[1] + tile, span : span + 1],
                     )
 
         def turn_half(pair, half):

@@ -25,6 +25,7 @@ BANKS_FOR_TRANSPOSES = 4
 BANKS_FOR_PRODUCTS = 4
 CAST_HALVES = {pair: 1 if pair[1] == 0 else 2 for pair in PAIRS if pair[0] == "y"}
 SCALAR_HALF = (("x", 3), 1)
+ALIGN = 256
 LOAD_AHEAD = 3
 
 
@@ -85,8 +86,8 @@ def tile_localised_ensemble_covariance_d4_kernel(tc, x_bytes, x_scale, y_bytes, 
         x_scales = keep.tile([P, 8, 8], F32, name="x_scales")
         nc.scalar.dma_start(out=x_scales[:], in_=x_scale.rearrange("(p i) k -> p i k", p=P))
 
-        h_codes = keep.tile([P, 4, 2 * R], U8, name="h_codes", align_bytes=64)
-        h_plane = keep.tile([P, 4, R], U8, name="h_plane", align_bytes=64)
+        h_codes = keep.tile([P, 4, 2 * R], U8, name="h_codes", align_bytes=ALIGN)
+        h_plane = keep.tile([P, 4, R], U8, name="h_plane", align_bytes=ALIGN)
         zeros = keep.tile([P, 320], F32, name="zeros")
         nc.vector.memset(zeros[:], 0.0)
         warm = psum.tile([P, 320], F32, name="bank")
@@ -96,7 +97,7 @@ def tile_localised_ensemble_covariance_d4_kernel(tc, x_bytes, x_scale, y_bytes, 
 
         for repeat in range(2):
             warm_up(320)
-        identity = keep.tile([P, P], F32, name="identity")
+        identity = keep.tile([P, P], F32, name="identity", align_bytes=ALIGN)
         nc.vector.memset(identity[:], 0.0)
         make_identity(nc, identity[:], nomemset=True)
         nc.vector.memset(h_plane[:].bitcast(I32), 0)
@@ -147,8 +148,8 @@ def tile_localised_ensemble_covariance_d4_kernel(tc, x_bytes, x_scale, y_bytes, 
         planes = {}
 
         def operand(key, shape):
-            codes[key] = keep.tile(shape, U32, name="codes_" + label(key), align_bytes=64)
-            planes[key] = keep.tile(shape, U8, name="plane_" + label(key), align_bytes=64)
+            codes[key] = keep.tile(shape, U32, name="codes_" + label(key), align_bytes=ALIGN)
+            planes[key] = keep.tile(shape, U8, name="plane_" + label(key), align_bytes=ALIGN)
 
         for pair in PAIRS:
             operand(pair, [P, 2, 256])
@@ -156,7 +157,7 @@ def tile_localised_ensemble_covariance_d4_kernel(tc, x_bytes, x_scale, y_bytes, 
         for q in range(4):
             operand(("z", q), [P, 4, 256])
             for g in range(4):
-                z_grouped[q, g] = keep.tile([P, 2, P, 4], BF16, name=f"z_grouped{q}{g}", align_bytes=64)
+                z_grouped[q, g] = keep.tile([P, 2, P, 4], BF16, name=f"z_grouped{q}{g}", align_bytes=ALIGN)
 
         plain = {}
         in_order = {}
@@ -169,7 +170,7 @@ def tile_localised_ensemble_covariance_d4_kernel(tc, x_bytes, x_scale, y_bytes, 
                 widen_on_scalar(*SCALAR_HALF)
             if pair[0] == "y":
                 width = 512 * CAST_HALVES[pair]
-                plain[pair] = stage.tile([P, 2, M], BF16, name="plain", align_bytes=64)
+                plain[pair] = stage.tile([P, 2, M], BF16, name="plain", align_bytes=ALIGN)
                 if width == M:
                     nc.scalar.copy(out=plain[pair][:], in_=raw[pair][:].bitcast(FP8))
                 else:
@@ -177,7 +178,7 @@ def tile_localised_ensemble_covariance_d4_kernel(tc, x_bytes, x_scale, y_bytes, 
                         nc.scalar.copy(out=plain[pair][:, e, :width], in_=raw[pair][:, e, :width].bitcast(FP8))
 
         def scale(pair, half):
-            scaled[pair, half] = stage.tile([P, 2, 2, 256], BF16, name=f"scaled{half}", align_bytes=64)
+            scaled[pair, half] = stage.tile([P, 2, 2, 256], BF16, name=f"scaled{half}", align_bytes=ALIGN)
             by_span = scaled[pair, half][:].rearrange("r w tile (b j c) -> r j tile b w c", j=4, b=4)
             if (pair, half) in in_order:
                 for tile in range(2):
@@ -210,7 +211,7 @@ def tile_localised_ensemble_covariance_d4_kernel(tc, x_bytes, x_scale, y_bytes, 
                     )
 
         def widen_on_scalar(pair, half):
-            in_order[pair, half] = keep.tile([P, 2, 512], BF16, name="in_order", align_bytes=64)
+            in_order[pair, half] = keep.tile([P, 2, 512], BF16, name="in_order", align_bytes=ALIGN)
             for tile in range(2):
                 for j in range(4):
                     span = 4 * half + j
@@ -230,7 +231,7 @@ def tile_localised_ensemble_covariance_d4_kernel(tc, x_bytes, x_scale, y_bytes, 
             half_banks[pair, half] = bank
 
         def empty_half(pair, half):
-            grouped[pair, half] = stage.tile([P, 256, 4], BF16, name=f"grouped{half}", align_bytes=64)
+            grouped[pair, half] = stage.tile([P, 256, 4], BF16, name=f"grouped{half}", align_bytes=ALIGN)
             words = grouped[pair, half][:].bitcast(F32)
             bank = half_banks[pair, half]
             if pair[0] == "x":
@@ -266,7 +267,7 @@ def tile_localised_ensemble_covariance_d4_kernel(tc, x_bytes, x_scale, y_bytes, 
             c_banks[q, g, u] = acc
 
         def localise(q, g, u):
-            z = z_pool.tile([P, 2, 256], BF16, name=f"z{u}", align_bytes=64)
+            z = z_pool.tile([P, 2, 256], BF16, name=f"z{u}", align_bytes=ALIGN)
             nc.vector.scalar_tensor_tensor(
                 out=z[:].rearrange("r a (p e) -> r (a p) e", e=2),
                 in0=c_banks[q, g, u][:].rearrange("r a (p e) -> r (a p) e", e=2),

@@ -237,7 +237,9 @@ def tile_localised_ensemble_covariance_d4_kernel(tc, x_bytes, x_scale, y_bytes, 
             if pair[0] == "x":
                 nc.scalar.copy(out=words.rearrange("p (a r) w -> p a r w", a=2), in_=bank[:].rearrange("p a w r -> p a r w"))
             else:
-                nc.scalar.copy(out=words.rearrange("p (r e) w -> p r e w", e=2), in_=bank[:].rearrange("p e w r -> p r e w"))
+                nc.scalar.copy(
+                    out=words.rearrange("p (s r e) w -> p s e r w", r=2, e=2), in_=bank[:].rearrange("p e w (s r) -> p s e r w", r=2)
+                )
 
         def quantise_half(pair, half):
             nc.vector.quantize_mx(

@@ -70,6 +70,9 @@ def panels_at(step):
     return [panel for panel in PANELS if PANEL_STEP[panel] == step and step < LAST_STEP]
 
 
+ON_GPSIMD = [products_at(LAST_STEP - 2)[0], products_at(LAST_STEP - 1)[-1]]
+
+
 def label(key):
     return "".join(str(part) for part in key)
 
@@ -270,15 +273,22 @@ def tile_localised_ensemble_covariance_d4_kernel(tc, x_bytes, x_scale, y_bytes, 
 
         def localise(q, g, u):
             z = z_pool.tile([P, 2, 256], BF16, name=f"z{u}", align_bytes=ALIGN)
+            z_tiles[q, g, u] = z
+            result = z[:].rearrange("r a (p e) -> r (a p) e", e=2)
+            factor = weights[q, g][:].rearrange("r a (p u e) -> r u (a p) e", u=2, e=2)[:, u]
+            if (q, g, u) in ON_GPSIMD:
+                c = keep.tile([P, 2, 256], F32, name=f"c{q}")
+                nc.scalar.activation(out=c[:], in_=c_banks[q, g, u][:], func=mybir.ActivationFunctionType.Copy, scale=1.0 / (M - 1))
+                nc.gpsimd.tensor_tensor(out=result, in0=c[:].rearrange("r a (p e) -> r (a p) e", e=2), in1=factor, op=MULT)
+                return
             nc.vector.scalar_tensor_tensor(
-                out=z[:].rearrange("r a (p e) -> r (a p) e", e=2),
+                out=result,
                 in0=c_banks[q, g, u][:].rearrange("r a (p e) -> r (a p) e", e=2),
                 scalar=1.0 / (M - 1),
-                in1=weights[q, g][:].rearrange("r a (p u e) -> r u (a p) e", u=2, e=2)[:, u],
+                in1=factor,
                 op0=MULT,
                 op1=MULT,
             )
-            z_tiles[q, g, u] = z
 
         def turn_panel(q, g):
             bank = psum.tile([P, 2, 2, P], F32, name="bank")

@@ -23,7 +23,7 @@ TURN_STEP = {pair: n if n < 2 else n - 1 for n, pair in enumerate(PAIRS)}
 BANKS = 8
 BANKS_FOR_TRANSPOSES = 4
 BANKS_FOR_PRODUCTS = 4
-CAST_HALVES = {pair: 1 if pair[1] == 0 else 2 for pair in PAIRS if pair[0] == "y"}
+CAST_HALVES = {pair: 1 if pair[1] == 0 or pair[1:] == (1, 1) else 2 for pair in PAIRS if pair[0] == "y"}
 SCALAR_HALF = (("x", 3), 1)
 ALIGN = 256
 LOAD_AHEAD = 3
@@ -51,6 +51,12 @@ PANEL_STEP = spread_over_steps(
 )
 
 
+PARKED_PANEL = (0, 0)
+FULL_STEPS = [step + 1 for step in range(LAST_STEP) if list(PRODUCT_STEP.values()).count(step) == BANKS_FOR_PRODUCTS]
+UNPARK_STEP = {PARKED_PANEL + (u,): FULL_STEPS[u] for u in range(2)}
+OUT_ORDER = [1, 2, 3, 0]
+
+
 def pairs_at(step):
     return [pair for pair in PAIRS if TURN_STEP[pair] == step]
 
@@ -67,7 +73,7 @@ def products_at(step):
 
 
 def panels_at(step):
-    return [panel for panel in PANELS if PANEL_STEP[panel] == step and step < LAST_STEP]
+    return [panel for panel in PANELS if PANEL_STEP[panel] == step and step < LAST_STEP and panel != PARKED_PANEL]
 
 
 ON_GPSIMD = [products_at(LAST_STEP - 2)[0], products_at(LAST_STEP - 1)[-1]]
@@ -234,7 +240,10 @@ def tile_localised_ensemble_covariance_d4_kernel(tc, x_bytes, x_scale, y_bytes, 
             half_banks[pair, half] = bank
 
         def empty_half(pair, half):
-            grouped[pair, half] = stage.tile([P, 256, 4], BF16, name=f"grouped{half}", align_bytes=ALIGN)
+            if half == 1 and TURN_STEP[pair] + 1 in UNPARK_STEP.values():
+                grouped[pair, half] = keep.tile([P, 256, 4], BF16, name="grouped_" + label(pair), align_bytes=ALIGN)
+            else:
+                grouped[pair, half] = stage.tile([P, 256, 4], BF16, name=f"grouped{half}", align_bytes=ALIGN)
             words = grouped[pair, half][:].bitcast(F32)
             bank = half_banks[pair, half]
             if pair[0] == "x":
@@ -254,6 +263,7 @@ def tile_localised_ensemble_covariance_d4_kernel(tc, x_bytes, x_scale, y_bytes, 
         c_banks = {}
         z_tiles = {}
         z_banks = {}
+        parked = {}
 
         def first_product(q, g, u):
             acc = psum.tile([P, 2, 256], F32, name="bank")
@@ -271,30 +281,38 @@ def tile_localised_ensemble_covariance_d4_kernel(tc, x_bytes, x_scale, y_bytes, 
                     )
             c_banks[q, g, u] = acc
 
+        def in_pairs(tile):
+            return tile.rearrange("r a (p e) -> r (a p) e", e=2)
+
+        def factor(q, g, u):
+            return weights[q, g][:].rearrange("r a (p u e) -> r u (a p) e", u=2, e=2)[:, u]
+
+        def park(q, g, u):
+            parked[q, g, u] = keep.tile([P, 2, 256], F32, name=f"parked{u}")
+            nc.scalar.activation(
+                out=parked[q, g, u][:], in_=c_banks[q, g, u][:], func=mybir.ActivationFunctionType.Copy, scale=1.0 / (M - 1)
+            )
+
+        def unpark(q, g, u, z):
+            z_tiles[q, g, u] = z
+            nc.gpsimd.tensor_tensor(out=in_pairs(z), in0=in_pairs(parked[q, g, u][:]), in1=factor(q, g, u), op=MULT)
+
         def localise(q, g, u):
             z = z_pool.tile([P, 2, 256], BF16, name=f"z{u}", align_bytes=ALIGN)
-            z_tiles[q, g, u] = z
-            result = z[:].rearrange("r a (p e) -> r (a p) e", e=2)
-            factor = weights[q, g][:].rearrange("r a (p u e) -> r u (a p) e", u=2, e=2)[:, u]
             if (q, g, u) in ON_GPSIMD:
-                c = keep.tile([P, 2, 256], F32, name=f"c{q}")
-                nc.scalar.activation(out=c[:], in_=c_banks[q, g, u][:], func=mybir.ActivationFunctionType.Copy, scale=1.0 / (M - 1))
-                nc.gpsimd.tensor_tensor(out=result, in0=c[:].rearrange("r a (p e) -> r (a p) e", e=2), in1=factor, op=MULT)
+                park(q, g, u)
+                unpark(q, g, u, z[:])
                 return
+            z_tiles[q, g, u] = z[:]
             nc.vector.scalar_tensor_tensor(
-                out=result,
-                in0=c_banks[q, g, u][:].rearrange("r a (p e) -> r (a p) e", e=2),
-                scalar=1.0 / (M - 1),
-                in1=factor,
-                op0=MULT,
-                op1=MULT,
+                out=in_pairs(z[:]), in0=in_pairs(c_banks[q, g, u][:]), scalar=1.0 / (M - 1), in1=factor(q, g, u), op0=MULT, op1=MULT
             )
 
         def turn_panel(q, g):
             bank = psum.tile([P, 2, 2, P], F32, name="bank")
             for a in range(2):
                 for u in range(2):
-                    nc.tensor.transpose(bank[:, a, u, :], z_tiles[q, g, u][:].bitcast(F32)[:, a, :], identity[:])
+                    nc.tensor.transpose(bank[:, a, u, :], z_tiles[q, g, u].bitcast(F32)[:, a, :], identity[:])
             z_banks[q, g] = bank
 
         def empty_panel(q, g):
@@ -356,8 +374,13 @@ def tile_localised_ensemble_covariance_d4_kernel(tc, x_bytes, x_scale, y_bytes, 
             nc.scalar.copy(out=y_scales[32 * quad : 32 * quad + 32, :, :], in_=spread[32 * quad : 32 * quad + 32, :, quad, :])
 
         for step in range(LAST_STEP + 1):
+            for product in UNPARK_STEP:
+                if UNPARK_STEP[product] == step:
+                    freed = grouped[pairs_at(step - 1)[-1], 1]
+                    unpark(*product, freed[:, :P, :].rearrange("r (a c) t -> r a (c t)", a=2))
             for product in products_at(step - 1):
-                localise(*product)
+                if product not in UNPARK_STEP:
+                    localise(*product)
             for pair, half in halves_at(step + 1):
                 scale(pair, half)
             for n, (pair, half) in enumerate(halves_at(step)):
@@ -370,6 +393,9 @@ def tile_localised_ensemble_covariance_d4_kernel(tc, x_bytes, x_scale, y_bytes, 
                 empty_half(pair, half)
             for panel in panels_at(step):
                 empty_panel(*panel)
+            for product in products_at(step - 1):
+                if product in UNPARK_STEP:
+                    park(*product)
             for pair in pairs_at(step + 2):
                 cast(pair)
             for product in products_at(step):
@@ -379,15 +405,17 @@ def tile_localised_ensemble_covariance_d4_kernel(tc, x_bytes, x_scale, y_bytes, 
 
         for product in products_at(LAST_STEP):
             localise(*product)
-        quantise_z(0, (0, 1))
-        for q in range(4):
-            for g in (2, 3):
-                turn_panel(q, g)
-                empty_panel(q, g)
-        quantise_z(0, (2, 3))
-        for q in (1, 2, 3):
+        quantise_z(OUT_ORDER[0], (0, 1))
+        for q in OUT_ORDER:
+            for g in range(4):
+                if g >= 2 or (q, g) == PARKED_PANEL:
+                    turn_panel(q, g)
+                    empty_panel(q, g)
+        quantise_z(OUT_ORDER[0], (2, 3))
+        for q in OUT_ORDER[1:]:
             quantise_z(q, range(4))
-        for i in range(7):
+        tiles = [2 * q + a for q in OUT_ORDER for a in range(2)]
+        for i in tiles[:-1]:
             second_product(i, range(4))
             store(i)
-        last_tile(7)
+        last_tile(tiles[-1])

@@ -54,7 +54,7 @@ PANEL_STEP = spread_over_steps(
 PARKED_PANEL = (0, 0)
 FULL_STEPS = [step + 1 for step in range(LAST_STEP) if list(PRODUCT_STEP.values()).count(step) == BANKS_FOR_PRODUCTS]
 UNPARK_STEP = {PARKED_PANEL + (u,): FULL_STEPS[u] for u in range(2)}
-OUT_ORDER = [1, 2, 3, 0]
+PANEL_STEP[PARKED_PANEL] = max(UNPARK_STEP.values()) + 1
 
 
 def pairs_at(step):
@@ -73,7 +73,7 @@ def products_at(step):
 
 
 def panels_at(step):
-    return [panel for panel in PANELS if PANEL_STEP[panel] == step and step < LAST_STEP and panel != PARKED_PANEL]
+    return [panel for panel in PANELS if PANEL_STEP[panel] == step and step < LAST_STEP]
 
 
 ON_GPSIMD = [products_at(LAST_STEP - 2)[0], products_at(LAST_STEP - 1)[-1]]
@@ -405,17 +405,15 @@ def tile_localised_ensemble_covariance_d4_kernel(tc, x_bytes, x_scale, y_bytes, 
 
         for product in products_at(LAST_STEP):
             localise(*product)
-        quantise_z(OUT_ORDER[0], (0, 1))
-        for q in OUT_ORDER:
-            for g in range(4):
-                if g >= 2 or (q, g) == PARKED_PANEL:
-                    turn_panel(q, g)
-                    empty_panel(q, g)
-        quantise_z(OUT_ORDER[0], (2, 3))
-        for q in OUT_ORDER[1:]:
+        quantise_z(0, (0, 1))
+        for q in range(4):
+            for g in (2, 3):
+                turn_panel(q, g)
+                empty_panel(q, g)
+        quantise_z(0, (2, 3))
+        for q in (1, 2, 3):
             quantise_z(q, range(4))
-        tiles = [2 * q + a for q in OUT_ORDER for a in range(2)]
-        for i in tiles[:-1]:
+        for i in range(7):
             second_product(i, range(4))
             store(i)
-        last_tile(tiles[-1])
+        last_tile(7)

@@ -51,7 +51,7 @@ PANEL_STEP = spread_over_steps(
 )
 
 
-PARKED_PANEL = (0, 0)
+PARKED_PANEL = (1, 0)
 FULL_STEPS = [step + 1 for step in range(LAST_STEP) if list(PRODUCT_STEP.values()).count(step) == BANKS_FOR_PRODUCTS]
 UNPARK_STEP = {PARKED_PANEL + (u,): FULL_STEPS[u] for u in range(2)}
 PANEL_STEP[PARKED_PANEL] = max(UNPARK_STEP.values()) + 1
@@ -94,6 +94,8 @@ def tile_localised_ensemble_covariance_d4_kernel(tc, x_bytes, x_scale, y_bytes, 
 
         x_scales = keep.tile([P, 8, 8], F32, name="x_scales")
         nc.scalar.dma_start(out=x_scales[:], in_=x_scale.rearrange("(p i) k -> p i k", p=P))
+        y_scale_column = keep.tile([P, 1], F32, name="y_scale_column")
+        nc.scalar.dma_start(out=y_scale_column[:], in_=y_scale.rearrange("b (k one) -> (b k) one", one=1))
 
         h_codes = keep.tile([P, 4, 2 * R], U8, name="h_codes", align_bytes=ALIGN)
         h_plane = keep.tile([P, 4, R], U8, name="h_plane", align_bytes=ALIGN)
@@ -133,8 +135,6 @@ def tile_localised_ensemble_covariance_d4_kernel(tc, x_bytes, x_scale, y_bytes, 
 
         load_half(("x", 0), 0)
         load_half(("y", 0, 0), 0)
-        y_scale_column = keep.tile([P, 1], F32, name="y_scale_column")
-        nc.sync.dma_start(out=y_scale_column[:], in_=y_scale.rearrange("b (k one) -> (b k) one", one=1))
         load_half(("x", 0), 1)
         load_half(("x", 1), 0)
         load_half(("y", 0, 0), 1)
@@ -267,17 +267,17 @@ def tile_localised_ensemble_covariance_d4_kernel(tc, x_bytes, x_scale, y_bytes, 
 
         def first_product(q, g, u):
             acc = psum.tile([P, 2, 256], F32, name="bank")
-            for a in range(2):
-                rows = slice(128 * a, 128 * a + 128)
-                for half in range(2):
+            for half in range(2):
+                for a in range(2):
+                    rows = slice(128 * a, 128 * a + 128)
                     nc.tensor.matmul_mx(
                         out=acc[:, a, :],
                         lhsT=codes["x", q][:, half, rows].bitcast(FP8X4),
                         lhsT_scale=planes["x", q][:, half, rows],
                         rhs=codes["y", g, u][:, half, :].bitcast(FP8X4),
                         rhs_scale=planes["y", g, u][:, half, :],
-                        start=(half == 0),
-                        stop=(half == 1),
+                        start=(half == 0 and a == 0),
+                        stop=(half == 1 and a == 1),
                     )
             c_banks[q, g, u] = acc
 
@@ -379,7 +379,9 @@ def tile_localised_ensemble_covariance_d4_kernel(tc, x_bytes, x_scale, y_bytes, 
                     freed = grouped[pairs_at(step - 1)[-1], 1]
                     unpark(*product, freed[:, :P, :].rearrange("r (a c) t -> r a (c t)", a=2))
             for product in products_at(step - 1):
-                if product not in UNPARK_STEP:
+                if product in UNPARK_STEP:
+                    park(*product)
+                else:
                     localise(*product)
             for pair, half in halves_at(step + 1):
                 scale(pair, half)
@@ -393,15 +395,13 @@ def tile_localised_ensemble_covariance_d4_kernel(tc, x_bytes, x_scale, y_bytes, 
                 empty_half(pair, half)
             for panel in panels_at(step):
                 empty_panel(*panel)
-            for product in products_at(step - 1):
-                if product in UNPARK_STEP:
-                    park(*product)
             for pair in pairs_at(step + 2):
                 cast(pair)
             for product in products_at(step):
                 first_product(*product)
-            for pair, half in halves_at(step):
-                quantise_half(pair, half)
+            for pair in pairs_at(step):
+                for half in range(2):
+                    quantise_half(pair, half)
 
         for product in products_at(LAST_STEP):
             localise(*product)

@@ -23,8 +23,7 @@ TURN_STEP = {pair: n if n < 2 else n - 1 for n, pair in enumerate(PAIRS)}
 BANKS = 8
 BANKS_FOR_TRANSPOSES = 4
 BANKS_FOR_PRODUCTS = 4
-CAST_HALVES = {pair: 1 if pair[1] == 0 or pair[1:] == (1, 1) else 2 for pair in PAIRS if pair[0] == "y"}
-SCALAR_HALF = (("x", 3), 1)
+CAST_HALVES = {pair: 2 if pair[1] == 3 or pair[1:] == (1, 0) else 1 for pair in PAIRS if pair[0] == "y"}
 ALIGN = 256
 LOAD_AHEAD = 3
 
@@ -51,10 +50,13 @@ PANEL_STEP = spread_over_steps(
 )
 
 
-PARKED_PANEL = (1, 0)
+GPSIMD_PANEL = (2, 0)
+LATE_PANELS = [(1, 0), (1, 1)]
+OUT_ORDER = [0, 2, 3, 1]
 FULL_STEPS = [step + 1 for step in range(LAST_STEP) if list(PRODUCT_STEP.values()).count(step) == BANKS_FOR_PRODUCTS]
-UNPARK_STEP = {PARKED_PANEL + (u,): FULL_STEPS[u] for u in range(2)}
-PANEL_STEP[PARKED_PANEL] = max(UNPARK_STEP.values()) + 1
+UNPARK_STEP = {GPSIMD_PANEL + (u,): FULL_STEPS[u] for u in range(2)}
+PANEL_STEP[GPSIMD_PANEL] = max(UNPARK_STEP.values()) + 1
+PARKED = [panel + (u,) for panel in LATE_PANELS + [GPSIMD_PANEL] for u in range(2)]
 
 
 def pairs_at(step):
@@ -69,11 +71,12 @@ def halves_at(step):
 
 
 def products_at(step):
-    return [product for product in PRODUCTS if PRODUCT_STEP[product] == step]
+    products = [product for product in PRODUCTS if PRODUCT_STEP[product] == step]
+    return sorted(products, key=lambda product: OUT_ORDER.index(product[0]) if product[1] == 3 else 0)
 
 
 def panels_at(step):
-    return [panel for panel in PANELS if PANEL_STEP[panel] == step and step < LAST_STEP]
+    return [panel for panel in PANELS if PANEL_STEP[panel] == step and step < LAST_STEP and panel not in LATE_PANELS]
 
 
 ON_GPSIMD = [products_at(LAST_STEP - 2)[0], products_at(LAST_STEP - 1)[-1]]
@@ -130,7 +133,7 @@ def tile_localised_ensemble_covariance_d4_kernel(tc, x_bytes, x_scale, y_bytes, 
             load_pair(pair, slice(512 * half, 512 * half + 512))
 
         def load_weights(q, g):
-            weights[q, g] = keep.tile([P, 2, 512], BF16, name=f"rho_{q}{g}")
+            weights[q, g] = keep.tile([P, 2, 512], BF16, name=f"rho_{q}{g}", align_bytes=ALIGN)
             nc.sync.dma_start(out=weights[q, g][:], in_=rho_rows[q][:, :, 512 * g : 512 * g + 512])
 
         load_half(("x", 0), 0)
@@ -169,14 +172,11 @@ def tile_localised_ensemble_covariance_d4_kernel(tc, x_bytes, x_scale, y_bytes, 
                 z_grouped[q, g] = keep.tile([P, 2, P, 4], BF16, name=f"z_grouped{q}{g}", align_bytes=ALIGN)
 
         plain = {}
-        in_order = {}
         scaled = {}
         half_banks = {}
         grouped = {}
 
         def cast(pair):
-            if pair == SCALAR_HALF[0]:
-                widen_on_scalar(*SCALAR_HALF)
             if pair[0] == "y":
                 width = 512 * CAST_HALVES[pair]
                 plain[pair] = stage.tile([P, 2, M], BF16, name="plain", align_bytes=ALIGN)
@@ -189,13 +189,6 @@ def tile_localised_ensemble_covariance_d4_kernel(tc, x_bytes, x_scale, y_bytes, 
         def scale(pair, half):
             scaled[pair, half] = stage.tile([P, 2, 2, 256], BF16, name=f"scaled{half}", align_bytes=ALIGN)
             by_span = scaled[pair, half][:].rearrange("r w tile (b j c) -> r j tile b w c", j=4, b=4)
-            if (pair, half) in in_order:
-                for tile in range(2):
-                    nc.vector.tensor_copy(
-                        out=by_span[:, :, tile],
-                        in_=in_order[pair, half][:, tile].rearrange("r (j b w c) -> r j b w c", j=4, b=4, w=2),
-                    )
-                return
             if half < CAST_HALVES.get(pair, 0):
                 for j in range(4):
                     span = 4 * half + j
@@ -217,18 +210,6 @@ def tile_localised_ensemble_covariance_d4_kernel(tc, x_bytes, x_scale, y_bytes, 
                         scalar1=factors[:, span : span + 1],
                         scalar2=None,
                         op0=MULT,
-                    )
-
-        def widen_on_scalar(pair, half):
-            in_order[pair, half] = keep.tile([P, 2, 512], BF16, name="in_order", align_bytes=ALIGN)
-            for tile in range(2):
-                for j in range(4):
-                    span = 4 * half + j
-                    nc.scalar.activation(
-                        out=in_order[pair, half][:, tile, 128 * j : 128 * j + 128],
-                        in_=raw[pair][:, tile, 128 * span : 128 * span + 128].bitcast(FP8),
-                        func=mybir.ActivationFunctionType.Copy,
-                        scale=x_scales[:, 2 * pair[1] + tile, span : span + 1],
                     )
 
         def turn_half(pair, half):
@@ -288,20 +269,24 @@ def tile_localised_ensemble_covariance_d4_kernel(tc, x_bytes, x_scale, y_bytes, 
             return weights[q, g][:].rearrange("r a (p u e) -> r u (a p) e", u=2, e=2)[:, u]
 
         def park(q, g, u):
-            parked[q, g, u] = keep.tile([P, 2, 256], F32, name=f"parked{u}")
+            name = f"parked{g}{u}" if (q, g) in LATE_PANELS else f"parked{u}"
+            if (q, g, u) == LATE_PANELS[1] + (0,):
+                parked[q, g, u] = keep.tile([P, 2, 256], F32, name=name, tag="rho_00", align_bytes=ALIGN)
+            else:
+                parked[q, g, u] = keep.tile([P, 2, 256], F32, name=name)
             nc.scalar.activation(
                 out=parked[q, g, u][:], in_=c_banks[q, g, u][:], func=mybir.ActivationFunctionType.Copy, scale=1.0 / (M - 1)
             )
 
-        def unpark(q, g, u, z):
+        def unpark(engine, q, g, u, z):
             z_tiles[q, g, u] = z
-            nc.gpsimd.tensor_tensor(out=in_pairs(z), in0=in_pairs(parked[q, g, u][:]), in1=factor(q, g, u), op=MULT)
+            engine.tensor_tensor(out=in_pairs(z), in0=in_pairs(parked[q, g, u][:]), in1=factor(q, g, u), op=MULT)
 
         def localise(q, g, u):
             z = z_pool.tile([P, 2, 256], BF16, name=f"z{u}", align_bytes=ALIGN)
             if (q, g, u) in ON_GPSIMD:
                 park(q, g, u)
-                unpark(q, g, u, z[:])
+                unpark(nc.gpsimd, q, g, u, z[:])
                 return
             z_tiles[q, g, u] = z[:]
             nc.vector.scalar_tensor_tensor(
@@ -348,7 +333,7 @@ def tile_localised_ensemble_covariance_d4_kernel(tc, x_bytes, x_scale, y_bytes, 
                 second_pass(sums[i][:], i, g, 0, R)
 
         def store(i):
-            rows = keep.tile([P, R], F32, name=f"out_rows{i}")
+            rows = stage.tile([P, R], F32, name="out_rows", bufs=4)
             nc.scalar.copy(out=rows[:], in_=sums[i][:])
             nc.sync.dma_start(out=out_rows[i], in_=rows[:])
 
@@ -357,7 +342,7 @@ def tile_localised_ensemble_covariance_d4_kernel(tc, x_bytes, x_scale, y_bytes, 
                 acc = psum.tile([P, 256], F32, name="bank")
                 for g in range(4):
                     second_pass(acc[:], i, g, 256 * side, 256)
-                columns = keep.tile([P, 256], F32, name=f"last_columns{side}")
+                columns = keep.tile([P, 256], F32, name=f"last_columns{side}", tag=f"parked{side}")
                 if side == 0:
                     nc.scalar.copy(out=columns[:], in_=acc[:])
                 else:
@@ -377,9 +362,9 @@ def tile_localised_ensemble_covariance_d4_kernel(tc, x_bytes, x_scale, y_bytes, 
             for product in UNPARK_STEP:
                 if UNPARK_STEP[product] == step:
                     freed = grouped[pairs_at(step - 1)[-1], 1]
-                    unpark(*product, freed[:, :P, :].rearrange("r (a c) t -> r a (c t)", a=2))
+                    unpark(nc.gpsimd, *product, freed[:, :P, :].rearrange("r (a c) t -> r a (c t)", a=2))
             for product in products_at(step - 1):
-                if product in UNPARK_STEP:
+                if product in PARKED:
                     park(*product)
                 else:
                     localise(*product)
@@ -405,15 +390,36 @@ def tile_localised_ensemble_covariance_d4_kernel(tc, x_bytes, x_scale, y_bytes, 
 
         for product in products_at(LAST_STEP):
             localise(*product)
-        quantise_z(0, (0, 1))
-        for q in range(4):
+        first, second, third, last = OUT_ORDER
+
+        def unpark_late(q, g):
+            for u in range(2):
+                z = keep.tile([P, 2, 256], BF16, name=f"late_z{g}{u}", tag=f"rho_{third}{2 * g + u}", align_bytes=ALIGN)
+                unpark(nc.vector, q, g, u, z[:])
+
+        def out_tiles(q):
+            for i in (2 * q, 2 * q + 1):
+                second_product(i, range(4))
+                store(i)
+
+        quantise_z(first, (0, 1))
+        for q in OUT_ORDER:
             for g in (2, 3):
                 turn_panel(q, g)
                 empty_panel(q, g)
-        quantise_z(0, (2, 3))
-        for q in (1, 2, 3):
-            quantise_z(q, range(4))
-        for i in range(7):
-            second_product(i, range(4))
-            store(i)
-        last_tile(7)
+        quantise_z(first, (2, 3))
+        unpark_late(*LATE_PANELS[0])
+        quantise_z(second, range(4))
+        out_tiles(first)
+        unpark_late(*LATE_PANELS[1])
+        out_tiles(second)
+        for panel in LATE_PANELS:
+            turn_panel(*panel)
+        for panel in LATE_PANELS:
+            empty_panel(*panel)
+        quantise_z(third, range(4))
+        quantise_z(last, (2, 3, 0, 1))
+        out_tiles(third)
+        second_product(2 * last, range(4))
+        store(2 * last)
+        last_tile(2 * last + 1)

@@ -23,9 +23,8 @@ TURN_STEP = {pair: n if n < 2 else n - 1 for n, pair in enumerate(PAIRS)}
 BANKS = 8
 BANKS_FOR_TRANSPOSES = 4
 BANKS_FOR_PRODUCTS = 4
-CAST_HALVES = {pair: 2 if pair[1] == 3 or pair[1:] == (1, 0) else 1 for pair in PAIRS if pair[0] == "y"}
+CAST_SPANS = {pair: 8 if pair[1] == 3 else 4 + pair[2] for pair in PAIRS if pair[0] == "y"}
 ALIGN = 256
-LOAD_AHEAD = 3
 
 
 def spread_over_steps(earliest, room):
@@ -43,20 +42,18 @@ PRODUCT_STEP = spread_over_steps(
 )
 PRODUCTS = sorted(PRODUCT_STEP, key=PRODUCT_STEP.get)
 LAST_STEP = max(PRODUCT_STEP.values())
-PANELS = sorted(((q, g) for g in range(4) for q in range(4)), key=lambda panel: PRODUCT_STEP[panel + (1,)])
-PANEL_STEP = spread_over_steps(
-    [(panel, PRODUCT_STEP[panel + (1,)] + 2) for panel in PANELS],
-    lambda step: BANKS_FOR_TRANSPOSES - (2 if step in TURN_STEP.values() else 0),
-)
-
-
 GPSIMD_PANEL = (2, 0)
 LATE_PANELS = [(1, 0), (1, 1)]
 OUT_ORDER = [0, 2, 3, 1]
 FULL_STEPS = [step + 1 for step in range(LAST_STEP) if list(PRODUCT_STEP.values()).count(step) == BANKS_FOR_PRODUCTS]
 UNPARK_STEP = {GPSIMD_PANEL + (u,): FULL_STEPS[u] for u in range(2)}
-PANEL_STEP[GPSIMD_PANEL] = max(UNPARK_STEP.values()) + 1
 PARKED = [panel + (u,) for panel in LATE_PANELS + [GPSIMD_PANEL] for u in range(2)]
+PANELS = sorted(((q, g) for g in range(4) for q in range(4)), key=lambda panel: PRODUCT_STEP[panel + (1,)])
+PANEL_STEP = spread_over_steps(
+    [(panel, PRODUCT_STEP[panel + (1,)] + 2) for panel in PANELS if panel + (0,) not in PARKED],
+    lambda step: 1 if step == LAST_STEP - 2 else BANKS_FOR_TRANSPOSES - 2,
+)
+PANEL_STEP[GPSIMD_PANEL] = max(UNPARK_STEP.values()) + 1
 
 
 def pairs_at(step):
@@ -76,10 +73,14 @@ def products_at(step):
 
 
 def panels_at(step):
-    return [panel for panel in PANELS if PANEL_STEP[panel] == step and step < LAST_STEP and panel not in LATE_PANELS]
+    return [panel for panel in PANELS if PANEL_STEP.get(panel) == step and step < LAST_STEP and panel[1] < 2]
 
 
 ON_GPSIMD = [products_at(LAST_STEP - 2)[0], products_at(LAST_STEP - 1)[-1]]
+
+
+def group_order(q):
+    return sorted(range(4), key=lambda g: (q, g) in LATE_PANELS)
 
 
 def label(key):
@@ -120,35 +121,47 @@ def tile_localised_ensemble_covariance_d4_kernel(tc, x_bytes, x_scale, y_bytes, 
         y_rows = y_bytes.rearrange("(g p u e) k -> g u p e k", p=P, u=2, e=2)
         rho_rows = rho.rearrange("(p q a) n -> q p a n", a=2, p=P)
         out_rows = out.rearrange("(p i) r -> i p r", p=P)
-        raw = {}
         weights = {}
+        raw = {}
 
-        def load_pair(pair, members=slice(0, M)):
-            if pair not in raw:
-                raw[pair] = keep.tile([P, 2, M], U8, name="raw_" + label(pair))
-            rows = x_rows[pair[1]] if pair[0] == "x" else y_rows[pair[1], pair[2]]
-            nc.sync.dma_start(out=raw[pair][:, :, members], in_=rows[:, :, members])
+        def load_x(q, members=slice(0, M)):
+            if ("x", q) not in raw:
+                raw["x", q] = keep.tile([P, 2, M], U8, name=f"raw_x{q}")
+            nc.sync.dma_start(out=raw["x", q][:, :, members], in_=x_rows[q][:, :, members])
 
-        def load_half(pair, half):
-            load_pair(pair, slice(512 * half, 512 * half + 512))
+        def load_y(pair, part):
+            cut = 128 * CAST_SPANS[pair]
+            members = slice(0, cut) if part == "cast" else slice(cut, M)
+            raw[pair, part] = keep.tile([P, 2, members.stop - members.start], U8, name=f"raw_{label(pair)}_{part}")
+            nc.sync.dma_start(out=raw[pair, part][:], in_=y_rows[pair[1], pair[2]][:, :, members])
 
         def load_weights(q, g):
             weights[q, g] = keep.tile([P, 2, 512], BF16, name=f"rho_{q}{g}", align_bytes=ALIGN)
             nc.sync.dma_start(out=weights[q, g][:], in_=rho_rows[q][:, :, 512 * g : 512 * g + 512])
 
-        load_half(("x", 0), 0)
-        load_half(("y", 0, 0), 0)
-        load_half(("x", 0), 1)
-        load_half(("x", 1), 0)
-        load_half(("y", 0, 0), 1)
-        load_half(("x", 1), 1)
-        for step in range(-LOAD_AHEAD, LAST_STEP + 1):
-            for pair in pairs_at(step + LOAD_AHEAD):
-                if pair not in raw:
-                    load_pair(pair)
-            for q, g, u in products_at(step):
-                if (q, g) not in weights:
+        first_half, second_half = slice(0, 512), slice(512, M)
+        load_x(0, first_half)
+        load_y(("y", 0, 0), "cast")
+        load_x(0, second_half)
+        load_x(1, first_half)
+        load_y(("y", 0, 0), "rest")
+        load_x(1, second_half)
+        for step in range(LAST_STEP + 1):
+            for q, g, u in products_at(step - 1):
+                if (q, g) not in weights and (q, g, u) not in PARKED:
                     load_weights(q, g)
+            if step == min(UNPARK_STEP.values()):
+                load_weights(*GPSIMD_PANEL)
+            for pair in pairs_at(step + 1):
+                if step > 0 and pair[0] == "x":
+                    load_x(pair[1])
+                elif step > 0 and CAST_SPANS[pair] < 8:
+                    load_y(pair, "rest")
+            for pair in pairs_at(step + 2):
+                if pair[0] == "y":
+                    load_y(pair, "cast")
+        for panel in LATE_PANELS:
+            load_weights(*panel)
         nc.sync.dma_start(out=h_codes[:].bitcast(I32), in_=h_words.rearrange("g p c -> p g c").bitcast(I32))
         for quad in range(4):
             nc.sync.dma_start(
@@ -178,39 +191,36 @@ def tile_localised_ensemble_covariance_d4_kernel(tc, x_bytes, x_scale, y_bytes, 
 
         def cast(pair):
             if pair[0] == "y":
-                width = 512 * CAST_HALVES[pair]
-                plain[pair] = stage.tile([P, 2, M], BF16, name="plain", align_bytes=ALIGN)
-                if width == M:
-                    nc.scalar.copy(out=plain[pair][:], in_=raw[pair][:].bitcast(FP8))
-                else:
-                    for e in range(2):
-                        nc.scalar.copy(out=plain[pair][:, e, :width], in_=raw[pair][:, e, :width].bitcast(FP8))
+                plain[pair] = stage.tile([P, 2, 128 * CAST_SPANS[pair]], BF16, name="plain", align_bytes=ALIGN)
+                nc.scalar.copy(out=plain[pair][:], in_=raw[pair, "cast"][:].bitcast(FP8))
 
         def scale(pair, half):
             scaled[pair, half] = stage.tile([P, 2, 2, 256], BF16, name=f"scaled{half}", align_bytes=ALIGN)
             by_span = scaled[pair, half][:].rearrange("r w tile (b j c) -> r j tile b w c", j=4, b=4)
-            if half < CAST_HALVES.get(pair, 0):
-                for j in range(4):
-                    span = 4 * half + j
+            spans = range(4 * half, 4 * half + 4)
+            cast_spans = CAST_SPANS.get(pair, 0)
+            for span in spans:
+                if span < cast_spans:
                     nc.vector.tensor_scalar(
-                        out=by_span[:, j],
+                        out=by_span[:, span % 4],
                         in0=plain[pair][:, :, 128 * span : 128 * span + 128].rearrange("r tile (b w c) -> r tile b w c", b=4, w=2),
                         scalar1=y_scales[:, pair[1], span : span + 1],
                         scalar2=None,
                         op0=MULT,
                     )
-                return
             for tile in range(2):
                 factors = x_scales[:, 2 * pair[1] + tile] if pair[0] == "x" else y_scales[:, pair[1]]
-                for j in range(4):
-                    span = 4 * half + j
-                    nc.vector.tensor_scalar(
-                        out=by_span[:, j, tile],
-                        in0=raw[pair][:, tile, 128 * span : 128 * span + 128].bitcast(FP8).rearrange("r (b w c) -> r b w c", b=4, w=2),
-                        scalar1=factors[:, span : span + 1],
-                        scalar2=None,
-                        op0=MULT,
-                    )
+                for span in spans:
+                    if span >= cast_spans:
+                        uncast = raw[pair] if pair[0] == "x" else raw[pair, "rest"]
+                        first = 128 * (span - cast_spans)
+                        nc.vector.tensor_scalar(
+                            out=by_span[:, span % 4, tile],
+                            in0=uncast[:, tile, first : first + 128].bitcast(FP8).rearrange("r (b w c) -> r b w c", b=4, w=2),
+                            scalar1=factors[:, span : span + 1],
+                            scalar2=None,
+                            op0=MULT,
+                        )
 
         def turn_half(pair, half):
             words = scaled[pair, half][:].bitcast(F32)
@@ -322,8 +332,8 @@ def tile_localised_ensemble_covariance_d4_kernel(tc, x_bytes, x_scale, y_bytes, 
                 lhsT_scale=planes["z", q][:, g, rows],
                 rhs=h_codes[:, g, 2 * first : 2 * (first + width)].bitcast(FP4X4),
                 rhs_scale=h_plane[:, g, first : first + width],
-                start=(g == 0),
-                stop=(g == 3),
+                start=(g == group_order(q)[0]),
+                stop=(g == group_order(q)[3]),
             )
 
         def second_product(i, groups):
@@ -340,7 +350,7 @@ def tile_localised_ensemble_covariance_d4_kernel(tc, x_bytes, x_scale, y_bytes, 
         def last_tile(i):
             for side in range(2):
                 acc = psum.tile([P, 256], F32, name="bank")
-                for g in range(4):
+                for g in group_order(i // 2):
                     second_pass(acc[:], i, g, 256 * side, 256)
                 columns = keep.tile([P, 256], F32, name=f"last_columns{side}", tag=f"parked{side}")
                 if side == 0:
@@ -418,8 +428,8 @@ def tile_localised_ensemble_covariance_d4_kernel(tc, x_bytes, x_scale, y_bytes, 
         for panel in LATE_PANELS:
             empty_panel(*panel)
         quantise_z(third, range(4))
-        quantise_z(last, (2, 3, 0, 1))
+        quantise_z(last, group_order(last))
         out_tiles(third)
-        second_product(2 * last, range(4))
+        second_product(2 * last, group_order(last))
         store(2 * last)
         last_tile(2 * last + 1)

@@ -107,11 +107,11 @@ def tile_localised_ensemble_covariance_d4_kernel(tc, x_bytes, x_scale, y_bytes, 
         nc.vector.memset(zeros[:], 0.0)
         warm = psum.tile([P, 320], F32, name="bank")
 
-        def warm_up(columns):
-            nc.tensor.matmul(warm[:, :columns], lhsT=zeros[:, :P], rhs=zeros[:, :columns], start=True, stop=True)
+        def warm_up(bank, columns):
+            nc.tensor.matmul(bank[:, :columns], lhsT=zeros[:, :P], rhs=zeros[:, :columns], start=True, stop=True)
 
-        for repeat in range(2):
-            warm_up(320)
+        warm_up(warm, 320)
+        warm_up(warm, 256)
         identity = keep.tile([P, P], F32, name="identity", align_bytes=ALIGN)
         nc.vector.memset(identity[:], 0.0)
         make_identity(nc, identity[:], nomemset=True)
@@ -225,6 +225,8 @@ def tile_localised_ensemble_covariance_d4_kernel(tc, x_bytes, x_scale, y_bytes, 
         def turn_half(pair, half):
             words = scaled[pair, half][:].bitcast(F32)
             bank = psum.tile([P, 2, 2, P], F32, name="bank")
+            if (pair, half) == (("x", 2), 1):
+                warm_up(bank[:].rearrange("p tile w r -> p (tile w r)"), 128)
             for tile in range(2):
                 for w in range(2):
                     nc.tensor.transpose(bank[:, tile, w, :], words[:, w, tile, :], identity[:])
@@ -383,7 +385,7 @@ def tile_localised_ensemble_covariance_d4_kernel(tc, x_bytes, x_scale, y_bytes, 
             for n, (pair, half) in enumerate(halves_at(step)):
                 turn_half(pair, half)
                 if step < 2 and n % 2 == 1:
-                    warm_up(192)
+                    warm_up(warm, 256 if n == 3 else 192)
             for panel in panels_at(step):
                 turn_panel(*panel)
             for pair, half in halves_at(step):

from contextlib import ExitStack

import concourse.mybir as mybir
from concourse.masks import make_identity

T, N, M, R = 1024, 2048, 1024, 512
P = 128
FLOPS = 2 * T * N * M + 2 * T * N * R

F32 = mybir.dt.float32
BF16 = mybir.dt.bfloat16
I32 = mybir.dt.int32
U32 = mybir.dt.uint32
U8 = mybir.dt.uint8
FP8 = mybir.dt.float8_e4m3fn
FP8X4 = mybir.dt.float8_e4m3fn_x4
FP4X4 = mybir.dt.float4_e2m1fn_x4
MULT = mybir.AluOpType.mult

PAIRS = [("x", 0), ("y", 0, 0), ("x", 1), ("y", 0, 1), ("x", 2), ("y", 1, 0), ("y", 1, 1), ("x", 3)]
PAIRS = PAIRS + [("y", g, u) for g in (2, 3) for u in range(2)]
TURN_STEP = {pair: n if n < 2 else n - 1 for n, pair in enumerate(PAIRS)}
BANKS = 8
BANKS_FOR_TRANSPOSES = 4
BANKS_FOR_PRODUCTS = 4
CAST_SPANS = {pair: 8 if pair[1] == 3 else 4 + pair[2] for pair in PAIRS if pair[0] == "y"}
ALIGN = 256


def spread_over_steps(earliest, room):
    steps = {}
    for item, step in earliest:
        while list(steps.values()).count(step) == room(step):
            step = step + 1
        steps[item] = step
    return steps


PRODUCT_STEP = spread_over_steps(
    [((q, g, u), max(TURN_STEP["x", q], TURN_STEP["y", g, u]) + 1) for g in range(4) for q in range(4) for u in range(2)],
    lambda step: BANKS_FOR_PRODUCTS,
)
PRODUCTS = sorted(PRODUCT_STEP, key=PRODUCT_STEP.get)
LAST_STEP = max(PRODUCT_STEP.values())
GPSIMD_PANEL = (2, 0)
LATE_PANELS = [(1, 0), (1, 1)]
OUT_ORDER = [0, 2, 3, 1]
FULL_STEPS = [step + 1 for step in range(LAST_STEP) if list(PRODUCT_STEP.values()).count(step) == BANKS_FOR_PRODUCTS]
UNPARK_STEP = {GPSIMD_PANEL + (u,): FULL_STEPS[u] for u in range(2)}
PARKED = [panel + (u,) for panel in LATE_PANELS + [GPSIMD_PANEL] for u in range(2)]
PANELS = sorted(((q, g) for g in range(4) for q in range(4)), key=lambda panel: PRODUCT_STEP[panel + (1,)])
PANEL_STEP = spread_over_steps(
    [(panel, PRODUCT_STEP[panel + (1,)] + 2) for panel in PANELS if panel + (0,) not in PARKED],
    lambda step: 1 if step == LAST_STEP - 2 else BANKS_FOR_TRANSPOSES - 2,
)
PANEL_STEP[GPSIMD_PANEL] = max(UNPARK_STEP.values()) + 1


def pairs_at(step):
    return [pair for pair in PAIRS if TURN_STEP[pair] == step]


def halves_at(step):
    halves = [(pair, half) for pair in pairs_at(step) for half in range(2)]
    if len(halves) == 4:
        return [halves[2], halves[0], halves[1], halves[3]]
    return halves


def products_at(step):
    products = [product for product in PRODUCTS if PRODUCT_STEP[product] == step]
    return sorted(products, key=lambda product: OUT_ORDER.index(product[0]) if product[1] == 3 else 0)


def panels_at(step):
    return [panel for panel in PANELS if PANEL_STEP.get(panel) == step and step < LAST_STEP and panel[1] < 2]


ON_GPSIMD = [products_at(LAST_STEP - 2)[0], products_at(LAST_STEP - 1)[-1]]


def group_order(q):
    return sorted(range(4), key=lambda g: (q, g) in LATE_PANELS)


def label(key):
    return "".join(str(part) for part in key)


def tile_localised_ensemble_covariance_d4_kernel(tc, x_bytes, x_scale, y_bytes, y_scale, rho, h_words, h_scales, out):
    nc = tc.nc
    with ExitStack() as ctx:
        keep = ctx.enter_context(tc.tile_pool(name="keep", bufs=1))
        stage = ctx.enter_context(tc.tile_pool(name="stage", bufs=3))
        z_pool = ctx.enter_context(tc.tile_pool(name="z_pool", bufs=8))
        psum = ctx.enter_context(tc.psum_pool(name="psum", bufs=BANKS))
        ctx.enter_context(tc.manual_schedule())

        x_scales = keep.tile([P, 8, 8], F32, name="x_scales")
        nc.scalar.dma_start(out=x_scales[:], in_=x_scale.rearrange("(p i) k -> p i k", p=P))
        y_scale_column = keep.tile([P, 1], F32, name="y_scale_column")
        nc.scalar.dma_start(out=y_scale_column[:], in_=y_scale.rearrange("b (k one) -> (b k) one", one=1))

        h_codes = keep.tile([P, 4, 2 * R], U8, name="h_codes", align_bytes=ALIGN)
        h_plane = keep.tile([P, 4, R], U8, name="h_plane", align_bytes=ALIGN)
        zeros = keep.tile([P, 320], F32, name="zeros")
        nc.vector.memset(zeros[:], 0.0)
        warm = psum.tile([P, 320], F32, name="bank")

        def warm_up(bank, columns):
            nc.tensor.matmul(bank[:, :columns], lhsT=zeros[:, :P], rhs=zeros[:, :columns], start=True, stop=True)

        warm_up(warm, 320)
        warm_up(warm, 256)
        identity = keep.tile([P, P], F32, name="identity", align_bytes=ALIGN)
        nc.vector.memset(identity[:], 0.0)
        make_identity(nc, identity[:], nomemset=True)
        nc.vector.memset(h_plane[:].bitcast(I32), 0)

        x_rows = x_bytes.rearrange("(p q a) k -> q p a k", a=2, p=P)
        y_rows = y_bytes.rearrange("(g p u e) k -> g u p e k", p=P, u=2, e=2)
        rho_rows = rho.rearrange("(p q a) n -> q p a n", a=2, p=P)
        out_rows = out.rearrange("(p i) r -> i p r", p=P)
        weights = {}
        raw = {}

        def load_x(q, members=slice(0, M)):
            if ("x", q) not in raw:
                raw["x", q] = keep.tile([P, 2, M], U8, name=f"raw_x{q}")
            nc.sync.dma_start(out=raw["x", q][:, :, members], in_=x_rows[q][:, :, members])

        def load_y(pair, part):
            cut = 128 * CAST_SPANS[pair]
            members = slice(0, cut) if part == "cast" else slice(cut, M)
            raw[pair, part] = keep.tile([P, 2, members.stop - members.start], U8, name=f"raw_{label(pair)}_{part}")
            nc.sync.dma_start(out=raw[pair, part][:], in_=y_rows[pair[1], pair[2]][:, :, members])

        def load_weights(q, g):
            weights[q, g] = keep.tile([P, 2, 512], BF16, name=f"rho_{q}{g}", align_bytes=ALIGN)
            nc.sync.dma_start(out=weights[q, g][:], in_=rho_rows[q][:, :, 512 * g : 512 * g + 512])

        first_half, second_half = slice(0, 512), slice(512, M)
        load_x(0, first_half)
        load_y(("y", 0, 0), "cast")
        load_x(0, second_half)
        load_x(1, first_half)
        load_y(("y", 0, 0), "rest")
        load_x(1, second_half)
        for step in range(LAST_STEP + 1):
            for q, g, u in products_at(step - 1):
                if (q, g) not in weights and (q, g, u) not in PARKED:
                    load_weights(q, g)
            if step == min(UNPARK_STEP.values()):
                load_weights(*GPSIMD_PANEL)
            for pair in pairs_at(step + 1):
                if step > 0 and pair[0] == "x":
                    load_x(pair[1])
                elif step > 0 and CAST_SPANS[pair] < 8:
                    load_y(pair, "rest")
            for pair in pairs_at(step + 2):
                if pair[0] == "y":
                    load_y(pair, "cast")
        for panel in LATE_PANELS:
            load_weights(*panel)
        nc.sync.dma_start(out=h_codes[:].bitcast(I32), in_=h_words.rearrange("g p c -> p g c").bitcast(I32))
        for quad in range(4):
            nc.sync.dma_start(
                out=h_plane[32 * quad : 32 * quad + 4, :, :].bitcast(I32),
                in_=h_scales[:, 4 * quad : 4 * quad + 4, :].rearrange("g r n -> r g n").bitcast(I32),
            )

        codes = {}
        planes = {}

        def operand(key, shape):
            codes[key] = keep.tile(shape, U32, name="codes_" + label(key), align_bytes=ALIGN)
            planes[key] = keep.tile(shape, U8, name="plane_" + label(key), align_bytes=ALIGN)

        for pair in PAIRS:
            operand(pair, [P, 2, 256])
        z_grouped = {}
        for q in range(4):
            operand(("z", q), [P, 4, 256])
            for g in range(4):
                z_grouped[q, g] = keep.tile([P, 2, P, 4], BF16, name=f"z_grouped{q}{g}", align_bytes=ALIGN)

        plain = {}
        scaled = {}
        half_banks = {}
        grouped = {}

        def cast(pair):
            if pair[0] == "y":
                plain[pair] = stage.tile([P, 2, 128 * CAST_SPANS[pair]], BF16, name="plain", align_bytes=ALIGN)
                nc.scalar.copy(out=plain[pair][:], in_=raw[pair, "cast"][:].bitcast(FP8))

        def scale(pair, half):
            scaled[pair, half] = stage.tile([P, 2, 2, 256], BF16, name=f"scaled{half}", align_bytes=ALIGN)
            by_span = scaled[pair, half][:].rearrange("r w tile (b j c) -> r j tile b w c", j=4, b=4)
            spans = range(4 * half, 4 * half + 4)
            cast_spans = CAST_SPANS.get(pair, 0)
            for span in spans:
                if span < cast_spans:
                    nc.vector.tensor_scalar(
                        out=by_span[:, span % 4],
                        in0=plain[pair][:, :, 128 * span : 128 * span + 128].rearrange("r tile (b w c) -> r tile b w c", b=4, w=2),
                        scalar1=y_scales[:, pair[1], span : span + 1],
                        scalar2=None,
                        op0=MULT,
                    )
            for tile in range(2):
                factors = x_scales[:, 2 * pair[1] + tile] if pair[0] == "x" else y_scales[:, pair[1]]
                for span in spans:
                    if span >= cast_spans:
                        uncast = raw[pair] if pair[0] == "x" else raw[pair, "rest"]
                        first = 128 * (span - cast_spans)
                        nc.vector.tensor_scalar(
                            out=by_span[:, span % 4, tile],
                            in0=uncast[:, tile, first : first + 128].bitcast(FP8).rearrange("r (b w c) -> r b w c", b=4, w=2),
                            scalar1=factors[:, span : span + 1],
                            scalar2=None,
                            op0=MULT,
                        )

        def turn_half(pair, half):
            words = scaled[pair, half][:].bitcast(F32)
            bank = psum.tile([P, 2, 2, P], F32, name="bank")
            if (pair, half) == (("x", 2), 1):
                warm_up(bank[:].rearrange("p tile w r -> p (tile w r)"), 128)
            for tile in range(2):
                for w in range(2):
                    nc.tensor.transpose(bank[:, tile, w, :], words[:, w, tile, :], identity[:])
            half_banks[pair, half] = bank

        def empty_half(pair, half):
            if half == 1 and TURN_STEP[pair] + 1 in UNPARK_STEP.values():
                grouped[pair, half] = keep.tile([P, 256, 4], BF16, name="grouped_" + label(pair), align_bytes=ALIGN)
            else:
                grouped[pair, half] = stage.tile([P, 256, 4], BF16, name=f"grouped{half}", align_bytes=ALIGN)
            words = grouped[pair, half][:].bitcast(F32)
            bank = half_banks[pair, half]
            if pair[0] == "x":
                nc.scalar.copy(out=words.rearrange("p (a r) w -> p a r w", a=2), in_=bank[:].rearrange("p a w r -> p a r w"))
            else:
                nc.scalar.copy(
                    out=words.rearrange("p (s r e) w -> p s e r w", r=2, e=2), in_=bank[:].rearrange("p e w (s r) -> p s e r w", r=2)
                )

        def quantise_half(pair, half):
            nc.vector.quantize_mx(
                out=codes[pair][:, half].bitcast(FP8X4),
                scales=planes[pair][:, half],
                in_=grouped[pair, half][:].rearrange("p r t -> p (r t)"),
            )

        c_banks = {}
        z_tiles = {}
        z_banks = {}
        parked = {}

        def first_product(q, g, u):
            acc = psum.tile([P, 2, 256], F32, name="bank")
            for half in range(2):
                for a in range(2):
                    rows = slice(128 * a, 128 * a + 128)
                    nc.tensor.matmul_mx(
                        out=acc[:, a, :],
                        lhsT=codes["x", q][:, half, rows].bitcast(FP8X4),
                        lhsT_scale=planes["x", q][:, half, rows],
                        rhs=codes["y", g, u][:, half, :].bitcast(FP8X4),
                        rhs_scale=planes["y", g, u][:, half, :],
                        start=(half == 0 and a == 0),
                        stop=(half == 1 and a == 1),
                    )
            c_banks[q, g, u] = acc

        def in_pairs(tile):
            return tile.rearrange("r a (p e) -> r (a p) e", e=2)

        def factor(q, g, u):
            return weights[q, g][:].rearrange("r a (p u e) -> r u (a p) e", u=2, e=2)[:, u]

        def park(q, g, u):
            name = f"parked{g}{u}" if (q, g) in LATE_PANELS else f"parked{u}"
            if (q, g, u) == LATE_PANELS[1] + (0,):
                parked[q, g, u] = keep.tile([P, 2, 256], F32, name=name, tag="rho_00", align_bytes=ALIGN)
            else:
                parked[q, g, u] = keep.tile([P, 2, 256], F32, name=name)
            nc.scalar.activation(
                out=parked[q, g, u][:], in_=c_banks[q, g, u][:], func=mybir.ActivationFunctionType.Copy, scale=1.0 / (M - 1)
            )

        def unpark(engine, q, g, u, z):
            z_tiles[q, g, u] = z
            engine.tensor_tensor(out=in_pairs(z), in0=in_pairs(parked[q, g, u][:]), in1=factor(q, g, u), op=MULT)

        def localise(q, g, u):
            z = z_pool.tile([P, 2, 256], BF16, name=f"z{u}", align_bytes=ALIGN)
            if (q, g, u) in ON_GPSIMD:
                park(q, g, u)
                unpark(nc.gpsimd, q, g, u, z[:])
                return
            z_tiles[q, g, u] = z[:]
            nc.vector.scalar_tensor_tensor(
                out=in_pairs(z[:]), in0=in_pairs(c_banks[q, g, u][:]), scalar=1.0 / (M - 1), in1=factor(q, g, u), op0=MULT, op1=MULT
            )

        def turn_panel(q, g):
            bank = psum.tile([P, 2, 2, P], F32, name="bank")
            for a in range(2):
                for u in range(2):
                    nc.tensor.transpose(bank[:, a, u, :], z_tiles[q, g, u].bitcast(F32)[:, a, :], identity[:])
            z_banks[q, g] = bank

        def empty_panel(q, g):
            nc.scalar.copy(out=z_grouped[q, g][:].bitcast(F32), in_=z_banks[q, g][:].rearrange("p a u r -> p a r u"))

        def quantise_z(q, groups):
            for g in groups:
                nc.vector.quantize_mx(
                    out=codes["z", q][:, g].bitcast(FP8X4),
                    scales=planes["z", q][:, g],
                    in_=z_grouped[q, g][:].rearrange("p a r t -> p (a r t)"),
                )

        sums = {}

        def second_pass(acc, i, g, first, width):
            q, a = divmod(i, 2)
            rows = slice(128 * a, 128 * a + 128)
            nc.tensor.matmul_mx(
                out=acc,
                lhsT=codes["z", q][:, g, rows].bitcast(FP8X4),
                lhsT_scale=planes["z", q][:, g, rows],
                rhs=h_codes[:, g, 2 * first : 2 * (first + width)].bitcast(FP4X4),
                rhs_scale=h_plane[:, g, first : first + width],
                start=(g == group_order(q)[0]),
                stop=(g == group_order(q)[3]),
            )

        def second_product(i, groups):
            if i not in sums:
                sums[i] = psum.tile([P, R], F32, name="bank")
            for g in groups:
                second_pass(sums[i][:], i, g, 0, R)

        def store(i):
            rows = stage.tile([P, R], F32, name="out_rows", bufs=4)
            nc.scalar.copy(out=rows[:], in_=sums[i][:])
            nc.sync.dma_start(out=out_rows[i], in_=rows[:])

        def last_tile(i):
            for side in range(2):
                acc = psum.tile([P, 256], F32, name="bank")
                for g in group_order(i // 2):
                    second_pass(acc[:], i, g, 256 * side, 256)
                columns = keep.tile([P, 256], F32, name=f"last_columns{side}", tag=f"parked{side}")
                if side == 0:
                    nc.scalar.copy(out=columns[:], in_=acc[:])
                else:
                    nc.vector.tensor_copy(out=columns[:], in_=acc[:])
                nc.sync.dma_start(out=out_rows[i][:, 256 * side : 256 * side + 256], in_=columns[:])

        for pair, half in halves_at(0):
            scale(pair, half)
        cast(("y", 0, 0))
        spread = psum.tile([P, 4, 4, 8], F32, name="bank")
        nc.tensor.transpose(spread[:].rearrange("p g quad k -> p (g quad k)"), y_scale_column[:].to_broadcast([P, P]), identity[:])
        y_scales = keep.tile([P, 4, 8], F32, name="y_scales")
        for quad in range(4):
            nc.scalar.copy(out=y_scales[32 * quad : 32 * quad + 32, :, :], in_=spread[32 * quad : 32 * quad + 32, :, quad, :])

        for step in range(LAST_STEP + 1):
            for product in UNPARK_STEP:
                if UNPARK_STEP[product] == step:
                    freed = grouped[pairs_at(step - 1)[-1], 1]
                    unpark(nc.gpsimd, *product, freed[:, :P, :].rearrange("r (a c) t -> r a (c t)", a=2))
            for product in products_at(step - 1):
                if product in PARKED:
                    park(*product)
                else:
                    localise(*product)
            for pair, half in halves_at(step + 1):
                scale(pair, half)
            for n, (pair, half) in enumerate(halves_at(step)):
                turn_half(pair, half)
                if step < 2 and n % 2 == 1:
                    warm_up(warm, 256 if n == 3 else 192)
            for panel in panels_at(step):
                turn_panel(*panel)
            for pair, half in halves_at(step):
                empty_half(pair, half)
            for panel in panels_at(step):
                empty_panel(*panel)
            for pair in pairs_at(step + 2):
                cast(pair)
            for product in products_at(step):
                first_product(*product)
            for pair in pairs_at(step):
                for half in range(2):
                    quantise_half(pair, half)

        for product in products_at(LAST_STEP):
            localise(*product)
        first, second, third, last = OUT_ORDER

        def unpark_late(q, g):
            for u in range(2):
                z = keep.tile([P, 2, 256], BF16, name=f"late_z{g}{u}", tag=f"rho_{third}{2 * g + u}", align_bytes=ALIGN)
                unpark(nc.vector, q, g, u, z[:])

        def out_tiles(q):
            for i in (2 * q, 2 * q + 1):
                second_product(i, range(4))
                store(i)

        quantise_z(first, (0, 1))
        for q in OUT_ORDER:
            for g in (2, 3):
                turn_panel(q, g)
                empty_panel(q, g)
        quantise_z(first, (2, 3))
        unpark_late(*LATE_PANELS[0])
        quantise_z(second, range(4))
        out_tiles(first)
        unpark_late(*LATE_PANELS[1])
        out_tiles(second)
        for panel in LATE_PANELS:
            turn_panel(*panel)
        for panel in LATE_PANELS:
            empty_panel(*panel)
        quantise_z(third, range(4))
        quantise_z(last, group_order(last))
        out_tiles(third)
        second_product(2 * last, group_order(last))
        store(2 * last)
        last_tile(2 * last + 1)
